import numpy as np
import ml_dtypes


def mxq(x, axis, fmt="e4m3"):
    dtype, down = {"e4m3": (ml_dtypes.float8_e4m3fn, 7), "e5m2": (ml_dtypes.float8_e5m2, 14)}[fmt]
    v = np.moveaxis(np.asarray(x, np.float32).astype(ml_dtypes.bfloat16).astype(np.float64), axis, -1)
    blocks = v.reshape(v.shape[:-1] + (-1, 32))
    amax = np.abs(blocks).max(-1, keepdims=True)
    byte = np.maximum(np.where(amax > 0, np.frexp(amax)[1] - 1 + 127, 0) - down, 1)
    scale = np.exp2(byte - 127.0)
    codes = (blocks / scale).astype(np.float32).astype(dtype).astype(np.float64)
    return np.moveaxis((codes * scale).reshape(v.shape), -1, axis)


WIDE = False


def mx_kscale(k):
    if not WIDE:
        return np.ones(k)
    levels = np.array([10, -10, 5, -5, 0])
    if k % 512:
        return np.exp2(np.random.permutation(np.resize(levels, k // 32))).repeat(32)
    a = np.empty((k // 512, 16))
    for p in range(k // 512):
        a[p, :8] = np.random.permutation(np.resize(levels, 8))
        for g in range(8):
            far = levels[np.abs(levels - a[p, g]) >= 10]
            a[p, g + 8] = far[np.random.randint(len(far))]
    return np.exp2(a.ravel()).repeat(32)


BF16 = ml_dtypes.bfloat16


def bf(x):
    return np.asarray(x, np.float32).astype(BF16)


def f64(x):
    return np.asarray(x).astype(np.float64)


B, HI, W, C, ND, P, O = 2, 4, 512, 1024, 512, 1024, 512


def softmax_last(t):
    e = np.exp(t - np.max(t, axis=-1, keepdims=True))
    return e / np.sum(e, axis=-1, keepdims=True)


def prime_context(x, wc, gw):
    y = mxq(f64(x), 3, "e4m3") @ mxq(f64(wc), 0, "e4m3")
    m = np.max(y, axis=1)
    centred = m - np.mean(m, axis=-1, keepdims=True)
    return centred * f64(gw)[None, :, None]


def prime_depth(dl, gd):
    n_depth = dl.shape[-1]
    return (n_depth * softmax_last(f64(dl))) * f64(gd)[None, None, :]


def draw0():
    s = mx_kscale(C)
    t = mx_kscale(ND)
    u = mx_kscale(W)
    return {
        "x": bf(np.random.standard_normal((B, HI, W, C)) * s),
        "wc": bf(np.random.standard_normal((C, O)) / np.sqrt(C) / s[:, None]),
        "gw": bf((1.0 + 0.1 * np.random.standard_normal(W)) / u),
        "dl": bf(1.5 * np.random.standard_normal((B, W, ND))),
        "gd": bf(np.random.standard_normal(ND) * t),
        "ring": bf(np.random.standard_normal((P, ND)) / np.sqrt(ND) / t[None, :]),
        "ray": bf(np.random.standard_normal((P, W)) / np.sqrt(W) * u[None, :]),
    }


def core(x, wc, gw, dl, gd, ring, ray):
    ctx = prime_context(x, wc, gw)
    d = prime_depth(dl, gd)
    rd = mxq(f64(ring), 1, "e4m3") @ mxq(d, 2, "e4m3").transpose(0, 2, 1)
    tm = rd * f64(ray)[None, :, :]
    return mxq(tm, 2, "e4m3") @ mxq(ctx, 1, "e4m3")


def e4m3fn_bytes(y):
    return np.clip(np.asarray(y, np.float64), -448.0, 448.0).astype(np.float32).astype(ml_dtypes.float8_e4m3fn).view(np.uint8)


def e4m3fn_values(b):
    return np.asarray(b, np.uint8).view(ml_dtypes.float8_e4m3fn).astype(np.float64)


def setup_inputs():
    d = draw0()
    x0 = np.asarray(d['x']).astype(np.float64)
    s = (np.max(np.abs(x0), axis=(0, 1, 2), keepdims=True) / 448.0).astype(np.float32)
    out = {}
    for k, v in d.items():
        if k == 'x':
            out['x_bytes'] = e4m3fn_bytes(x0 / s.astype(np.float64))
            out['x_scale'] = s
        else:
            out[k] = v
    return out


def reference(x_bytes, x_scale, wc, gw, dl, gd, ring, ray):
    return core(e4m3fn_values(x_bytes) * x_scale.astype(np.float64), wc, gw, dl, gd, ring, ray)

@@ -1,0 +1,392 @@
+from contextlib import ExitStack
+
+import concourse.mybir as mybir
+from concourse.masks import make_identity
+
+F32 = mybir.dt.float32
+BF16 = mybir.dt.bfloat16
+U32 = mybir.dt.uint32
+U8 = mybir.dt.uint8
+FP8 = mybir.dt.float8_e4m3fn
+FP8X4 = mybir.dt.float8_e4m3fn_x4
+ACT = mybir.ActivationFunctionType
+ALU = mybir.AluOpType
+AXIS = mybir.AxisListType
+
+B, HI, W, C, ND, NP, NO = 2, 4, 512, 1024, 512, 1024, 512
+P = 128
+
+FLOPS = 2 * B * HI * W * C * NO + 2 * B * NP * ND * W + 2 * B * NP * W * NO
+
+
+def tile_matrixvtringraybev_kernel(tc, x_bytes, x_scale, wc, gw, dl, gd, ring, ray, out):
+    nc = tc.nc
+    with ExitStack() as ctx:
+        keep = ctx.enter_context(tc.tile_pool(name="keep", bufs=1))
+        work = ctx.enter_context(tc.tile_pool(name="work", bufs=1))
+        psum = ctx.enter_context(tc.psum_pool(name="psum", bufs=1))
+        ctx.enter_context(tc.manual_schedule())
+
+        def sb(name, shape, dtype, bufs=1, pool=keep):
+            return pool.tile(shape, dtype, name=name, tag=name, bufs=bufs, align_bytes=64)
+
+        def bank(tag, bufs):
+            return psum.tile([P, 512], F32, name=tag, tag=tag, bufs=bufs)
+
+        def tp_bank():
+            return bank("tp", 3)
+
+        def o_bank():
+            return bank("o", 3)
+
+        ident = sb("ident", [P, P], F32)
+        make_identity(nc, ident[:])
+        warm = sb("warm", [P, 1], F32)
+        nc.vector.memset(warm[:], 0.0)
+
+        scol = sb("scol", [P, 2, 4], F32)
+        nc.sync.dma_start(out=scol[:], in_=x_scale.rearrange("a b c (h p t) -> p (a b c h) t", h=2, t=4))
+        gd_b = sb("gd_b", [P, 4], BF16)
+        nc.scalar.dma_start(out=gd_b[:], in_=gd.rearrange("(p t) -> p t", t=4))
+        gw_b = sb("gw_b", [P, 4], BF16)
+        nc.scalar.dma_start(out=gw_b[:], in_=gw.rearrange("(p t) -> p t", t=4))
+        nc.scalar.activation(out=warm[:], in_=warm[:], func=ACT.Exp)
+
+        wc_raw = [sb("wc_raw%d" % g, [P, 4, NO], BF16) for g in range(2)]
+        wc_v = wc.rearrange("(g p t) o -> g p t o", p=P, t=4)
+        xb = [[sb("xb%d%d" % (b, t), [P, HI, C], U8) for t in range(4)] for b in range(B)]
+        x_v = [x_bytes[b].rearrange("h (p t) k -> p t h k", t=4) for b in range(B)]
+        dl_raw = [sb("dl_raw%d" % b, [P, 4, ND], BF16) for b in range(B)]
+        dl_v = [dl[b].rearrange("(p t) n -> p t n", t=4) for b in range(B)]
+        ring_raw = sb("ring_raw", [P, 8, ND], BF16)
+        ray_raw = sb("ray_raw", [P, 8, W], BF16)
+
+        def load_x(b, t, h0, h1):
+            nc.sync.dma_start(out=xb[b][t][:, h0:h1, :], in_=x_v[b][:, t, h0:h1, :])
+
+        nc.sync.dma_start(out=wc_raw[0][:], in_=wc_v[0])
+        load_x(0, 0, 0, 2)
+        load_x(0, 0, 2, 4)
+        nc.sync.dma_start(out=wc_raw[1][:], in_=wc_v[1])
+        nc.sync.dma_start(out=dl_raw[0][:], in_=dl_v[0])
+        load_x(0, 1, 0, 4)
+        nc.sync.dma_start(out=ring_raw[:], in_=ring.rearrange("(p c) n -> p c n", c=8))
+        load_x(0, 2, 0, 4)
+        load_x(0, 3, 0, 4)
+        nc.sync.dma_start(out=ray_raw[:], in_=ray.rearrange("(p c) w -> p c w", c=8))
+        nc.sync.dma_start(out=dl_raw[1][:], in_=dl_v[1])
+        for t in range(4):
+            load_x(1, t, 0, 4)
+
+        scale = sb("scale", [P, C], F32)
+        for h in range(2):
+            sp = tp_bank()
+            for t in range(4):
+                nc.tensor.transpose(sp[:, t * P : (t + 1) * P], scol[:, h, t : t + 1].to_broadcast([P, P]), ident[:])
+            dst = scale[:, h * 512 : (h + 1) * 512].rearrange("q (p t) -> q p t", t=4)
+            src = sp[:].rearrange("q (t p) -> q p t", t=4)
+            if h == 0:
+                nc.vector.tensor_copy(out=dst, in_=src)
+            else:
+                nc.scalar.copy(out=dst, in_=src)
+
+        gd_f = sb("gd_f", [P, 4], F32)
+        nc.vector.tensor_copy(out=gd_f[:], in_=gd_b[:])
+        gw_f = sb("gw_f", [P, 4], F32)
+        nc.vector.tensor_copy(out=gw_f[:], in_=gw_b[:])
+        gd_row = sb("gd_row", [P, ND], F32)
+        gp = tp_bank()
+        for t in range(4):
+            nc.tensor.transpose(gp[:, t * P : (t + 1) * P], gd_f[:, t : t + 1].to_broadcast([P, P]), ident[:])
+        nc.scalar.activation(
+            out=gd_row[:].rearrange("q (p t) -> q p t", t=4),
+            in_=gp[:].rearrange("q (t p) -> q p t", t=4),
+            func=ACT.Copy,
+            scale=float(ND),
+        )
+
+        wq = sb("wq", [P, 2 * NO], U32)
+        wq_s = sb("wq_s", [P, 2 * NO], U8)
+        wg = [sb("wg%d" % g, [P, NO * 4], BF16) for g in range(2)]
+        nmax = [sb("nmax%d" % b, [P, 4], F32) for b in range(B)]
+        esum = [sb("esum%d" % b, [P, 4], F32) for b in range(B)]
+        rsum = [sb("rsum%d" % b, [P, 4], F32) for b in range(B)]
+        dg = [sb("dg%d" % b, [P, 4 * P * 4], BF16) for b in range(B)]
+        dq = [sb("dq%d" % b, [P, W], U32) for b in range(B)]
+        dq_s = [sb("dq_s%d" % b, [P, W], U8) for b in range(B)]
+        rg = sb("rg", [P, NP * 4], BF16)
+        rq = sb("rq", [P, NP], U32)
+        rq_s = sb("rq_s", [P, NP], U8)
+        rayg = sb("rayg", [P, NP * 4], BF16)
+        tmg = [[sb("tmg%d%d" % (b, i), [P, 2048], BF16) for i in range(2)] for b in range(B)]
+        tq = [[sb("tq%d%d" % (b, i), [P, 512], U32) for i in range(2)] for b in range(B)]
+        tq_s = [[sb("tq_s%d%d" % (b, i), [P, 512], U8) for i in range(2)] for b in range(B)]
+        msum = [[sb("msum%d%d" % (b, t), [P, 1], F32) for t in range(4)] for b in range(B)]
+        nbias = [[sb("nbias%d%d" % (b, t), [P, 1], F32) for t in range(4)] for b in range(B)]
+        cx = [sb("cx%d" % b, [P, 4, NO], BF16) for b in range(B)]
+        cg = [[sb("cg%d%d" % (b, i), [P, 1024], BF16) for i in range(2)] for b in range(B)]
+        cq = [[sb("cq%d%d" % (b, i), [P, 256], U32) for i in range(2)] for b in range(B)]
+        cq_s = [[sb("cq_s%d%d" % (b, i), [P, 256], U8) for i in range(2)] for b in range(B)]
+        e_t = {}
+        d_t = {}
+        m_t = {}
+        o_t = {}
+        xs_t = {}
+        xg_t = {}
+        xq_t = {}
+        y_t = {}
+
+        def quantize(codes, scales, src):
+            nc.vector.quantize_mx(out=codes.bitcast(FP8X4), scales=scales, in_=src)
+
+        def mx(dst, lhs, lhs_s, rhs, rhs_s, start=True, stop=True):
+            nc.tensor.matmul_mx(
+                out=dst, lhsT=lhs.bitcast(FP8X4), lhsT_scale=lhs_s, rhs=rhs.bitcast(FP8X4), rhs_scale=rhs_s, start=start, stop=stop
+            )
+
+        def wc_interleave(g):
+            nc.scalar.copy(out=wg[g][:].rearrange("p (o t) -> p o t", t=4), in_=wc_raw[g][:].rearrange("p t o -> p o t"))
+
+        def wc_quant(g):
+            quantize(wq[:, g * NO : (g + 1) * NO], wq_s[:, g * NO : (g + 1) * NO], wg[g][:])
+
+        def dmax(b):
+            src = dl_raw[b]
+            n = ND // 2
+            cur = src
+            while n >= 32:
+                nxt = sb("mx%d" % n, [P, 4, n], BF16, pool=work)
+                nc.vector.tensor_tensor(out=nxt[:], in0=cur[:, :, 0:n], in1=cur[:, :, n : 2 * n], op=ALU.max)
+                cur = nxt
+                n //= 2
+            top = sb("dtop", [P, 4], F32, pool=work)
+            nc.vector.tensor_reduce(out=top[:], in_=cur[:], axis=AXIS.X, op=ALU.max)
+            nc.vector.tensor_scalar(out=nmax[b][:], in0=top[:], scalar1=-1.0, scalar2=None, op0=ALU.mult)
+
+        def dexp(b):
+            for t in range(4):
+                e = sb("e", [P, ND], F32, bufs=5, pool=work)
+                nc.scalar.activation(
+                    out=e[:], in_=dl_raw[b][:, t, :], func=ACT.Exp, bias=nmax[b][:, t : t + 1], accum_out=esum[b][:, t : t + 1]
+                )
+                e_t[b, t] = e
+
+        def drecip(b):
+            nc.vector.reciprocal(out=rsum[b][:], in_=esum[b][:])
+
+        def dprod(b, t):
+            d = sb("d", [P, ND], BF16, bufs=4, pool=work)
+            nc.vector.scalar_tensor_tensor(
+                out=d[:], in0=e_t[b, t][:], scalar=rsum[b][:, t : t + 1], in1=gd_row[:], op0=ALU.mult, op1=ALU.mult
+            )
+            d_t[b, t] = d
+
+        def turn_pair(rows, dst):
+            bk = tp_bank()
+            for i in range(2):
+                words = rows[i].bitcast(F32)
+                for u in range(2):
+                    nc.tensor.transpose(bk[:, (2 * i + u) * P : (2 * i + u + 1) * P], words[:, u : 256 : 2], ident[:])
+            nc.scalar.copy(
+                out=dst.bitcast(F32).rearrange("p (i r u) -> p i r u", i=2, u=2),
+                in_=bk[:].rearrange("p (i u r) -> p i r u", i=2, u=2),
+            )
+
+        def d_turn(b, i):
+            turn_pair([d_t[b, 2 * i][:], d_t[b, 2 * i + 1][:]], dg[b][:, i * 1024 : (i + 1) * 1024])
+
+        def d_quant(b):
+            quantize(dq[b][:], dq_s[b][:], dg[b][:])
+
+        def ring_turn(i):
+            turn_pair([ring_raw[:, 2 * i, :], ring_raw[:, 2 * i + 1, :]], rg[:, i * 1024 : (i + 1) * 1024])
+
+        def ring_quant(i):
+            quantize(rq[:, i * 512 : (i + 1) * 512], rq_s[:, i * 512 : (i + 1) * 512], rg[:, i * 2048 : (i + 1) * 2048])
+
+        def ray_turn(i):
+            turn_pair([ray_raw[:, 2 * i, :], ray_raw[:, 2 * i + 1, :]], rayg[:, i * 1024 : (i + 1) * 1024])
+
+        def mm2(b, c):
+            o = o_bank()
+            for t in range(4):
+                sl = slice(t * P, (t + 1) * P)
+                cs = slice(c * P, (c + 1) * P)
+                mx(o[:, sl], dq[b][:, sl], dq_s[b][:, sl], rq[:, cs], rq_s[:, cs])
+            o_t[b, c] = o
+
+        def tm(b, c):
+            i, r = divmod(c, 4)
+            nc.vector.tensor_tensor(
+                out=tmg[b][i][:, r * 512 : (r + 1) * 512].rearrange("p (n t) -> p n t", t=4),
+                in0=o_t[b, c][:].rearrange("p (t n) -> p n t", t=4),
+                in1=rayg[:, c * 512 : (c + 1) * 512].rearrange("p (n t) -> p n t", t=4),
+                op=ALU.mult,
+            )
+
+        def tm_quant(b, i):
+            quantize(tq[b][i][:], tq_s[b][i][:], tmg[b][i][:])
+
+        def centre(b, t, eng):
+            nc.vector.tensor_scalar(
+                out=nbias[b][t][:], in0=msum[b][t][:], scalar1=-1.0 / NO, scalar2=gw_f[:, t : t + 1], op0=ALU.mult, op1=ALU.mult
+            )
+            if eng == "s":
+                nc.scalar.activation(out=cx[b][:, t, :], in_=m_t[b, t][:], func=ACT.Identity, bias=nbias[b][t][:], scale=gw_f[:, t : t + 1])
+            else:
+                nc.vector.tensor_scalar(
+                    out=cx[b][:, t, :], in0=m_t[b, t][:], scalar1=gw_f[:, t : t + 1], scalar2=nbias[b][t][:], op0=ALU.mult, op1=ALU.add
+                )
+
+        def ctx_interleave(b, i, eng):
+            dst = cg[b][i][:].rearrange("p (o t) -> p o t", t=4)
+            src = cx[b][:, :, i * 256 : (i + 1) * 256].rearrange("p t o -> p o t")
+            if eng == "s":
+                nc.scalar.copy(out=dst, in_=src)
+            else:
+                nc.vector.tensor_copy(out=dst, in_=src)
+
+        def ctx_quant(b, i):
+            quantize(cq[b][i][:], cq_s[b][i][:], cg[b][i][:])
+
+        out_v = [out[b].rearrange("(p c) o -> p c o", c=8) for b in range(B)]
+
+        def mm3(b, c, eng, bk):
+            i, r = divmod(c, 4)
+            sl = slice(r * P, (r + 1) * P)
+            for n in range(2):
+                mx(bk[:, n * 256 : (n + 1) * 256], tq[b][i][:, sl], tq_s[b][i][:, sl], cq[b][n][:], cq_s[b][n][:])
+            res = sb("res", [P, NO], F32, bufs=6, pool=work)
+            if eng == "s":
+                nc.scalar.copy(out=res[:], in_=bk[:])
+            else:
+                nc.vector.tensor_copy(out=res[:], in_=bk[:])
+            nc.sync.dma_start(out=out_v[b][:, c, :], in_=res[:])
+
+        def where(j):
+            return j // 8, (j // 2) % 4, 2 * (j % 2)
+
+        def x_mult(j):
+            b, t, h0 = where(j)
+            for i in range(2):
+                xs = sb("xs", [P, C], BF16, bufs=6, pool=work)
+                nc.vector.tensor_tensor(out=xs[:], in0=xb[b][t][:, h0 + i, :].bitcast(FP8), in1=scale[:], op=ALU.mult)
+                xs_t[j, i] = xs
+
+        def x_turn(j):
+            xg = sb("xg", [P, 2 * 2 * P * 4], BF16, bufs=3, pool=work)
+            xg_t[j] = xg
+            banks = []
+            for i in range(2):
+                bk = tp_bank()
+                words = xs_t[j, i][:].bitcast(F32)
+                for g in range(2):
+                    for u in range(2):
+                        s = 2 * g + u
+                        nc.tensor.transpose(bk[:, s * P : (s + 1) * P], words[:, 256 * g + u : 256 * (g + 1) : 2], ident[:])
+                banks.append(bk)
+            xw = xg[:].bitcast(F32)
+            for i in range(2):
+                nc.scalar.copy(
+                    out=xw[:, i * 512 : (i + 1) * 512].rearrange("p (g r u) -> p g r u", g=2, u=2),
+                    in_=banks[i][:].rearrange("p (g u r) -> p g r u", g=2, u=2),
+                )
+
+        def x_quant(j, parts=1):
+            codes = sb("xq", [P, 512], U32, bufs=3, pool=work)
+            scales = sb("xq_s", [P, 512], U8, bufs=3, pool=work)
+            n = 512 // parts
+            for i in range(parts):
+                quantize(codes[:, i * n : (i + 1) * n], scales[:, i * n : (i + 1) * n], xg_t[j][:, 4 * i * n : 4 * (i + 1) * n])
+            xq_t[j] = (codes, scales)
+
+        def mm1(j):
+            b, t, h0 = where(j)
+            codes, scales = xq_t[j]
+            ys = []
+            for i in range(2):
+                y = bank("y", 2)
+                for g in range(2):
+                    sl = slice((2 * i + g) * P, (2 * i + g + 1) * P)
+                    ocols = slice(g * NO, (g + 1) * NO)
+                    mx(y[:], codes[:, sl], scales[:, sl], wq[:, ocols], wq_s[:, ocols], start=g == 0, stop=g == 1)
+                ys.append(y)
+            y_t[j] = ys
+            if h0 == 0:
+                m = sb("m", [P, NO], F32, bufs=4, pool=work)
+                nc.scalar.copy(out=m[:], in_=ys[0][:])
+                m_t[b, t] = m
+
+        def y_max(j, eng="s"):
+            b, t, h0 = where(j)
+            m = m_t[b, t]
+            ys = y_t[j]
+            if h0 == 0:
+                nc.vector.tensor_tensor(out=m[:], in0=ys[1][:], in1=m[:], op=ALU.max)
+            else:
+                nc.vector.tensor_tensor(out=m[:], in0=ys[0][:], in1=m[:], op=ALU.max)
+                nc.vector.scalar_tensor_tensor(
+                    out=m[:], in0=ys[1][:], scalar=1.0, in1=m[:], op0=ALU.mult, op1=ALU.max, accum_out=msum[b][t][:]
+                )
+                centre(b, t, eng)
+
+        pre = {
+            1: [(wc_quant, 0), (wc_quant, 1)],
+            2: [(ring_turn, 0), (ring_turn, 1)],
+            3: [(d_turn, 0, 0), (d_turn, 0, 1), (ring_turn, 2), (ring_turn, 3)],
+            4: [(ray_turn, 0), (ray_turn, 1), (d_quant, 0)],
+            5: [(ray_turn, 2), (ray_turn, 3)],
+            7: [(d_turn, 1, 0), (d_turn, 1, 1)],
+        }
+        post = {
+            0: [(dmax, 0)],
+            1: [(dexp, 0)],
+            2: [(drecip, 0), (dprod, 0, 0), (dprod, 0, 1), (dprod, 0, 2), (dprod, 0, 3)],
+            3: [(ring_quant, 0), (dmax, 1)],
+            4: [(ring_quant, 1), (mm2, 0, 0), (mm2, 0, 1), (dexp, 1)],
+            5: [(tm, 0, 0), (tm, 0, 1), (mm2, 0, 2), (mm2, 0, 3), (drecip, 1), (dprod, 1, 0), (dprod, 1, 1)],
+            6: [(tm, 0, 2), (tm, 0, 3), (mm2, 0, 4), (mm2, 0, 5), (dprod, 1, 2), (dprod, 1, 3)],
+            7: [(tm, 0, 4), (tm, 0, 5), (mm2, 0, 6), (mm2, 0, 7), (tm_quant, 0, 0)],
+            8: [(tm, 0, 6), (tm, 0, 7), (d_quant, 1), (mm2, 1, 0), (mm2, 1, 1)],
+            9: [(tm_quant, 0, 1), (tm, 1, 0), (tm, 1, 1), (mm2, 1, 2), (mm2, 1, 3), (ctx_interleave, 0, 0, "s"), (ctx_interleave, 0, 1, "s")],
+            10: [(tm, 1, 2), (tm, 1, 3), (mm2, 1, 4), (mm2, 1, 5), (ctx_quant, 0, 0), (ctx_quant, 0, 1)],
+            11: [(tm, 1, 4), (tm, 1, 5), (mm2, 1, 6), (mm2, 1, 7), (tm_quant, 1, 0)],
+            12: [(tm, 1, 6), (tm, 1, 7)],
+            13: [(tm_quant, 1, 1)],
+        }
+
+        def run(items):
+            for item in items:
+                item[0](*item[1:])
+
+        def mm3_step(j):
+            if 12 <= j < 16:
+                for c in (2 * (j - 12), 2 * (j - 12) + 1):
+                    mm3(0, c, "s", o_bank())
+
+        n_pairs = 16
+        for j in range(n_pairs):
+            if j == 0:
+                wc_interleave(0)
+                wc_interleave(1)
+            x_mult(j)
+            if j >= 2:
+                y_max(j - 2)
+            if j >= 1:
+                x_quant(j - 1)
+            x_turn(j)
+            run(pre.get(j, []))
+            if j >= 1:
+                mm1(j - 1)
+            run(post.get(j, []))
+            mm3_step(j)
+        y_max(n_pairs - 2)
+        x_quant(n_pairs - 1, parts=2)
+        mm1(n_pairs - 1)
+        y_max(n_pairs - 1, "v")
+        ctx_interleave(1, 0, "v")
+        ctx_interleave(1, 1, "s")
+        ctx_quant(1, 0)
+        ctx_quant(1, 1)
+        for c in range(8):
+            mm3(1, c, "sv"[c % 2], o_bank() if c % 2 else tp_bank())

@@ -16,6 +16,82 @@ AXIS = mybir.AxisListType
 B, HI, W, C, ND, NP, NO = 2, 4, 512, 1024, 512, 1024, 512
 P = 128
 
+BY_SCALAR = [(1, 1, 0), (1, 3, 0)]
+PLAN = {
+    (0, 0): [('wi', 0)],
+    (0, 4): [('wi', 1)],
+    (1, 2): [('dmax', 0), ('wq', 0)],
+    (1, 3): [('dmax', 1), ('wq', 1)],
+    (1, 4): [('dmax', 2)],
+    (2, 0): [('ring', 3)],
+    (2, 1): [('dmax', 3)],
+    (2, 2): [('dmax', 4), ('ring', 2)],
+    (2, 4): [('dmax', 5)],
+    (3, 0): [('exp', 0, 2), ('exp', 0, 3)],
+    (3, 2): [('exp', 0, 1), ('ring', 1)],
+    (3, 3): [('exp', 0, 0)],
+    (4, 0): [('fc', 1, 1, 0, 0)],
+    (4, 1): [('ray', 0), ('ring', 0)],
+    (4, 3): [('fc', 1, 1, 0, 1), ('recip', 0)],
+    (4, 4): [('dprod', 0, 3)],
+    (5, 0): [('fc', 1, 1, 0, 3), ('dprod', 0, 0), ('dprod', 0, 1)],
+    (5, 1): [('dprod', 0, 2), ('dt', 0, 0)],
+    (5, 2): [('ray', 1), ('fc', 1, 1, 0, 2), ('ringq', 1)],
+    (5, 4): [('dt', 0, 1)],
+    (6, 2): [('ft', 1, 1, 0, 0), ('dq', 0), ('exp', 1, 3)],
+    (6, 3): [('fs', 1, 1, 0, 0), ('exp', 1, 2), ('exp', 1, 1)],
+    (6, 4): [('fs', 1, 1, 0, 1), ('mean', 0, 1)],
+    (7, 1): [('ft', 1, 1, 0, 1), ('exp', 1, 0)],
+    (7, 2): [('fs', 1, 1, 0, 2)],
+    (7, 3): [('fc', 1, 3, 0, 0), ('ringq', 0), ('mm2', 0, 0), ('recip', 1)],
+    (7, 4): [('fs', 1, 1, 0, 3), ('centre', 0, 1), ('dprod', 1, 0), ('mean', 0, 0), ('ray', 2)],
+    (8, 0): [('centre', 0, 0), ('dprod', 1, 1)],
+    (8, 2): [('fm', 1, 1, 0, 0), ('mean', 0, 2)],
+    (8, 3): [('mm2', 0, 1), ('fc', 1, 3, 0, 3)],
+    (8, 4): [('dt', 1, 0)],
+    (9, 1): [('tm', 0, 0)],
+    (9, 2): [('fc', 1, 3, 0, 2)],
+    (9, 3): [('dprod', 1, 3), ('fm', 1, 1, 0, 1)],
+    (9, 4): [('ray', 3), ('tm', 0, 1)],
+    (10, 1): [('mm2', 0, 2)],
+    (10, 2): [('fc', 1, 3, 0, 1), ('dprod', 1, 2)],
+    (10, 4): [('ft', 1, 3, 0, 0), ('fq', 1, 1, 0), ('centre', 0, 2), ('fs', 1, 3, 0, 0)],
+    (11, 0): [('fs', 1, 3, 0, 1)],
+    (11, 1): [('dt', 1, 1), ('mean', 0, 3)],
+    (11, 2): [('ft', 1, 3, 0, 1), ('tmq', 0, 0), ('fs', 1, 3, 0, 3)],
+    (11, 3): [('centre', 0, 3), ('fs', 1, 3, 0, 2)],
+    (11, 4): [('ci', 0, 1), ('mm2', 0, 3)],
+    (12, 1): [('tm', 0, 2), ('dq', 1)],
+    (12, 2): [('mm2', 0, 4), ('tm', 0, 3), ('ci', 0, 0)],
+    (12, 4): [('tm', 0, 4), ('tmq', 0, 1), ('mean', 1, 0)],
+    (13, 0): [('cq', 0, 1), ('mm2', 0, 5)],
+    (13, 1): [('centre', 1, 0), ('fm', 1, 3, 0, 0), ('cq', 0, 0)],
+    (13, 2): [('mm3', 0, 0)],
+    (13, 4): [('fm', 1, 3, 0, 1)],
+    (14, 1): [('mm2', 0, 7)],
+    (14, 2): [('mm3', 0, 3), ('tm', 0, 5)],
+    (14, 3): [('mm2', 0, 6)],
+    (14, 4): [('tm', 0, 7)],
+    (15, 0): [('mm3', 0, 2)],
+    (15, 3): [('fq', 1, 3, 0), ('mm3', 0, 1)],
+    (15, 4): [('tm', 0, 6), ('mm2', 1, 1)],
+    (16, 1): [('tmq', 0, 2), ('mm2', 1, 0), ('tmq', 0, 3)],
+    (16, 2): [('mean', 1, 1), ('mm3', 0, 7), ('mean', 1, 2)],
+    (16, 4): [('mm3', 0, 5), ('tm', 1, 0)],
+    (17, 0): [('tm', 1, 1)],
+    (17, 1): [('centre', 1, 2)],
+    (17, 2): [('centre', 1, 1), ('mm2', 1, 3)],
+    (17, 3): [('mm2', 1, 2), ('tmq', 1, 0)],
+    (17, 4): [('tm', 1, 2)],
+    (18, 0): [('mm3', 0, 4), ('tm', 1, 3)],
+    (18, 1): [('mm2', 1, 4), ('tm', 1, 4)],
+    (18, 2): [('mm3', 0, 6), ('mm2', 1, 5)],
+    (19, 0): [('tm', 1, 5), ('mm2', 1, 6)],
+    (20, 0): [('tmq', 1, 1), ('tmq', 1, 2), ('mm2', 1, 7), ('tm', 1, 7), ('tm', 1, 6)],
+    (25, 0): [('tmq', 1, 3)],
+}
+EV = "sssssssv"
+
 FLOPS = 2 * B * HI * W * C * NO + 2 * B * NP * ND * W + 2 * B * NP * W * NO
 
 
@@ -37,10 +113,18 @@ def tile_matrixvtringraybev_kernel(tc, x_bytes, x_scale, wc, gw, dl, gd, ring, r
             return bank("tp", 3)
 
         def o_bank():
-            return bank("o", 3)
+            return bank("o", 2)
+
+        def y_bank():
+            return bank("y", 2)
+
+        def r_bank():
+            return bank("r", 1)
 
         ident = sb("ident", [P, P], F32)
         make_identity(nc, ident[:])
+        ident_b = sb("ident_b", [P, P], BF16)
+        nc.gpsimd.tensor_copy(out=ident_b[:], in_=ident[:])
         warm = sb("warm", [P, 1], F32)
         nc.vector.memset(warm[:], 0.0)
 
@@ -52,29 +136,31 @@ def tile_matrixvtringraybev_kernel(tc, x_bytes, x_scale, wc, gw, dl, gd, ring, r
         nc.scalar.dma_start(out=gw_b[:], in_=gw.rearrange("(p t) -> p t", t=4))
         nc.scalar.activation(out=warm[:], in_=warm[:], func=ACT.Exp)
 
-        wc_raw = [sb("wc_raw%d" % g, [P, 4, NO], BF16) for g in range(2)]
+        wc_raw = [sb("wr", [P, 4, NO], BF16, bufs=2) for g in range(2)]
         wc_v = wc.rearrange("(g p t) o -> g p t o", p=P, t=4)
         xb = [[sb("xb%d%d" % (b, t), [P, HI, C], U8) for t in range(4)] for b in range(B)]
         x_v = [x_bytes[b].rearrange("h (p t) k -> p t h k", t=4) for b in range(B)]
-        dl_raw = [sb("dl_raw%d" % b, [P, 4, ND], BF16) for b in range(B)]
+        dl_raw = sb("dl_raw", [P, B * 4, ND], BF16)
         dl_v = [dl[b].rearrange("(p t) n -> p t n", t=4) for b in range(B)]
         ring_raw = sb("ring_raw", [P, 8, ND], BF16)
-        ray_raw = sb("ray_raw", [P, 8, W], BF16)
+        ray_raw = []
 
         def load_x(b, t, h0, h1):
             nc.sync.dma_start(out=xb[b][t][:, h0:h1, :], in_=x_v[b][:, t, h0:h1, :])
 
-        nc.sync.dma_start(out=wc_raw[0][:], in_=wc_v[0])
+        def load_dl(b):
+            nc.sync.dma_start(out=dl_raw[:, 4 * b : 4 * b + 4, :], in_=dl_v[b])
+
         load_x(0, 0, 0, 2)
+        nc.sync.dma_start(out=wc_raw[0][:], in_=wc_v[0])
         load_x(0, 0, 2, 4)
         nc.sync.dma_start(out=wc_raw[1][:], in_=wc_v[1])
-        nc.sync.dma_start(out=dl_raw[0][:], in_=dl_v[0])
+        load_dl(0)
+        load_dl(1)
         load_x(0, 1, 0, 4)
-        nc.sync.dma_start(out=ring_raw[:], in_=ring.rearrange("(p c) n -> p c n", c=8))
         load_x(0, 2, 0, 4)
+        nc.sync.dma_start(out=ring_raw[:], in_=ring.rearrange("(p c) n -> p c n", c=8))
         load_x(0, 3, 0, 4)
-        nc.sync.dma_start(out=ray_raw[:], in_=ray.rearrange("(p c) w -> p c w", c=8))
-        nc.sync.dma_start(out=dl_raw[1][:], in_=dl_v[1])
         for t in range(4):
             load_x(1, t, 0, 4)
 
@@ -107,18 +193,18 @@ def tile_matrixvtringraybev_kernel(tc, x_bytes, x_scale, wc, gw, dl, gd, ring, r
 
         wq = sb("wq", [P, 2 * NO], U32)
         wq_s = sb("wq_s", [P, 2 * NO], U8)
-        wg = [sb("wg%d" % g, [P, NO * 4], BF16) for g in range(2)]
-        nmax = [sb("nmax%d" % b, [P, 4], F32) for b in range(B)]
+        wg = {}
+        nmax = sb("nmax", [P, B * 4], F32)
         esum = [sb("esum%d" % b, [P, 4], F32) for b in range(B)]
         rsum = [sb("rsum%d" % b, [P, 4], F32) for b in range(B)]
-        dg = [sb("dg%d" % b, [P, 4 * P * 4], BF16) for b in range(B)]
+        dg = {}
         dq = [sb("dq%d" % b, [P, W], U32) for b in range(B)]
         dq_s = [sb("dq_s%d" % b, [P, W], U8) for b in range(B)]
         rg = sb("rg", [P, NP * 4], BF16)
         rq = sb("rq", [P, NP], U32)
         rq_s = sb("rq_s", [P, NP], U8)
         rayg = sb("rayg", [P, NP * 4], BF16)
-        tmg = [[sb("tmg%d%d" % (b, i), [P, 2048], BF16) for i in range(2)] for b in range(B)]
+        tmg = {}
         tq = [[sb("tq%d%d" % (b, i), [P, 512], U32) for i in range(2)] for b in range(B)]
         tq_s = [[sb("tq_s%d%d" % (b, i), [P, 512], U8) for i in range(2)] for b in range(B)]
         msum = [[sb("msum%d%d" % (b, t), [P, 1], F32) for t in range(4)] for b in range(B)]
@@ -145,31 +231,34 @@ def tile_matrixvtringraybev_kernel(tc, x_bytes, x_scale, wc, gw, dl, gd, ring, r
             )
 
         def wc_interleave(g):
+            wg[g] = sb("fg", [P, NO * 4], BF16, bufs=2, pool=work)
             nc.scalar.copy(out=wg[g][:].rearrange("p (o t) -> p o t", t=4), in_=wc_raw[g][:].rearrange("p t o -> p o t"))
 
         def wc_quant(g):
             quantize(wq[:, g * NO : (g + 1) * NO], wq_s[:, g * NO : (g + 1) * NO], wg[g][:])
 
-        def dmax(b):
-            src = dl_raw[b]
-            n = ND // 2
-            cur = src
-            while n >= 32:
-                nxt = sb("mx%d" % n, [P, 4, n], BF16, pool=work)
-                nc.vector.tensor_tensor(out=nxt[:], in0=cur[:, :, 0:n], in1=cur[:, :, n : 2 * n], op=ALU.max)
-                cur = nxt
-                n //= 2
-            top = sb("dtop", [P, 4], F32, pool=work)
-            nc.vector.tensor_reduce(out=top[:], in_=cur[:], axis=AXIS.X, op=ALU.max)
-            nc.vector.tensor_scalar(out=nmax[b][:], in0=top[:], scalar1=-1.0, scalar2=None, op0=ALU.mult)
+        lev = [dl_raw]
 
-        def dexp(b):
-            for t in range(4):
-                e = sb("e", [P, ND], F32, bufs=5, pool=work)
-                nc.scalar.activation(
-                    out=e[:], in_=dl_raw[b][:, t, :], func=ACT.Exp, bias=nmax[b][:, t : t + 1], accum_out=esum[b][:, t : t + 1]
-                )
-                e_t[b, t] = e
+        def dmax(i):
+            if i < 4:
+                n = ND >> (i + 1)
+                nxt = sb("lev%d" % i, [P, B * 4, n], BF16)
+                nc.vector.tensor_tensor(out=nxt[:], in0=lev[i][:, :, 0:n], in1=lev[i][:, :, n : 2 * n], op=ALU.max)
+                lev.append(nxt)
+            elif i == 4:
+                top = sb("dtop", [P, B * 4], F32)
+                nc.vector.tensor_reduce(out=top[:], in_=lev[4][:], axis=AXIS.X, op=ALU.max)
+                lev.append(top)
+            else:
+                nc.vector.tensor_scalar(out=nmax[:], in0=lev[5][:], scalar1=-1.0, scalar2=None, op0=ALU.mult)
+
+        def dexp(b, t):
+            e = sb("e", [P, ND], F32, bufs=4, pool=work)
+            r = 4 * b + t
+            nc.scalar.activation(
+                out=e[:], in_=dl_raw[:, r, :], func=ACT.Exp, bias=nmax[:, r : r + 1], accum_out=esum[b][:, t : t + 1]
+            )
+            e_t[b, t] = e
 
         def drecip(b):
             nc.vector.reciprocal(out=rsum[b][:], in_=esum[b][:])
@@ -193,6 +282,8 @@ def tile_matrixvtringraybev_kernel(tc, x_bytes, x_scale, wc, gw, dl, gd, ring, r
             )
 
         def d_turn(b, i):
+            if i == 0:
+                dg[b] = sb("dg", [P, 4 * P * 4], BF16)
             turn_pair([d_t[b, 2 * i][:], d_t[b, 2 * i + 1][:]], dg[b][:, i * 1024 : (i + 1) * 1024])
 
         def d_quant(b):
@@ -204,8 +295,15 @@ def tile_matrixvtringraybev_kernel(tc, x_bytes, x_scale, wc, gw, dl, gd, ring, r
         def ring_quant(i):
             quantize(rq[:, i * 512 : (i + 1) * 512], rq_s[:, i * 512 : (i + 1) * 512], rg[:, i * 2048 : (i + 1) * 2048])
 
+        def load_ray():
+            for i in range(2):
+                ray_raw.append(sb("wr", [P, 4, W], BF16, bufs=2))
+                nc.sync.dma_start(out=ray_raw[i][:], in_=ray.rearrange("(p c) w -> p c w", c=8)[:, 4 * i : 4 * i + 4, :])
+
         def ray_turn(i):
-            turn_pair([ray_raw[:, 2 * i, :], ray_raw[:, 2 * i + 1, :]], rayg[:, i * 1024 : (i + 1) * 1024])
+            half = ray_raw[i // 2]
+            c = 2 * (i % 2)
+            turn_pair([half[:, c, :], half[:, c + 1, :]], rayg[:, i * 1024 : (i + 1) * 1024])
 
         def mm2(b, c):
             o = o_bank()
@@ -217,20 +315,26 @@ def tile_matrixvtringraybev_kernel(tc, x_bytes, x_scale, wc, gw, dl, gd, ring, r
 
         def tm(b, c):
             i, r = divmod(c, 4)
+            if r == 0:
+                tmg[b, i] = sb("tmg", [P, 2048], BF16, bufs=2)
             nc.vector.tensor_tensor(
-                out=tmg[b][i][:, r * 512 : (r + 1) * 512].rearrange("p (n t) -> p n t", t=4),
+                out=tmg[b, i][:, r * 512 : (r + 1) * 512].rearrange("p (n t) -> p n t", t=4),
                 in0=o_t[b, c][:].rearrange("p (t n) -> p n t", t=4),
                 in1=rayg[:, c * 512 : (c + 1) * 512].rearrange("p (n t) -> p n t", t=4),
                 op=ALU.mult,
             )
 
-        def tm_quant(b, i):
-            quantize(tq[b][i][:], tq_s[b][i][:], tmg[b][i][:])
+        def tm_quant(b, q):
+            i, h = divmod(q, 2)
+            sl = slice(h * 256, (h + 1) * 256)
+            quantize(tq[b][i][:, sl], tq_s[b][i][:, sl], tmg[b, i][:, h * 1024 : (h + 1) * 1024])
 
-        def centre(b, t, eng):
-            nc.vector.tensor_scalar(
+        def negmean(b, t):
+            (nc.vector if (b, t) == (1, 3) else nc.gpsimd).tensor_scalar(
                 out=nbias[b][t][:], in0=msum[b][t][:], scalar1=-1.0 / NO, scalar2=gw_f[:, t : t + 1], op0=ALU.mult, op1=ALU.mult
             )
+
+        def centre(b, t, eng):
             if eng == "s":
                 nc.scalar.activation(out=cx[b][:, t, :], in_=m_t[b, t][:], func=ACT.Identity, bias=nbias[b][t][:], scale=gw_f[:, t : t + 1])
             else:
@@ -256,7 +360,7 @@ def tile_matrixvtringraybev_kernel(tc, x_bytes, x_scale, wc, gw, dl, gd, ring, r
             sl = slice(r * P, (r + 1) * P)
             for n in range(2):
                 mx(bk[:, n * 256 : (n + 1) * 256], tq[b][i][:, sl], tq_s[b][i][:, sl], cq[b][n][:], cq_s[b][n][:])
-            res = sb("res", [P, NO], F32, bufs=6, pool=work)
+            res = sb("res", [P, NO], F32, bufs=8, pool=work)
             if eng == "s":
                 nc.scalar.copy(out=res[:], in_=bk[:])
             else:
@@ -266,48 +370,106 @@ def tile_matrixvtringraybev_kernel(tc, x_bytes, x_scale, wc, gw, dl, gd, ring, r
         def where(j):
             return j // 8, (j // 2) % 4, 2 * (j % 2)
 
-        def x_mult(j):
+        def is_scalar(b, t, g):
+            return (b, t, g) in BY_SCALAR
+
+        def x_mult(j, i):
             b, t, h0 = where(j)
-            for i in range(2):
-                xs = sb("xs", [P, C], BF16, bufs=6, pool=work)
-                nc.vector.tensor_tensor(out=xs[:], in0=xb[b][t][:, h0 + i, :].bitcast(FP8), in1=scale[:], op=ALU.mult)
-                xs_t[j, i] = xs
+            cols = [g for g in range(2) if not is_scalar(b, t, g)]
+            if not cols:
+                return
+            lo, hi = cols[0] * 512, cols[-1] * 512 + 512
+            xs = sb("xs", [P, C], BF16, bufs=5, pool=work)
+            for c0, c1 in [(lo, 512), (512, hi)] if (j, i) == (0, 0) else [(lo, hi)]:
+                nc.vector.tensor_tensor(out=xs[:, c0:c1], in0=xb[b][t][:, h0 + i, c0:c1].bitcast(FP8), in1=scale[:, c0:c1], op=ALU.mult)
+            xs_t[j, i] = xs
 
-        def x_turn(j):
-            xg = sb("xg", [P, 2 * 2 * P * 4], BF16, bufs=3, pool=work)
-            xg_t[j] = xg
-            banks = []
-            for i in range(2):
-                bk = tp_bank()
-                words = xs_t[j, i][:].bitcast(F32)
-                for g in range(2):
-                    for u in range(2):
-                        s = 2 * g + u
-                        nc.tensor.transpose(bk[:, s * P : (s + 1) * P], words[:, 256 * g + u : 256 * (g + 1) : 2], ident[:])
-                banks.append(bk)
-            xw = xg[:].bitcast(F32)
-            for i in range(2):
-                nc.scalar.copy(
-                    out=xw[:, i * 512 : (i + 1) * 512].rearrange("p (g r u) -> p g r u", g=2, u=2),
-                    in_=banks[i][:].rearrange("p (g u r) -> p g r u", g=2, u=2),
-                )
+        def x_turn(j, i):
+            b, t, h0 = where(j)
+            cols = [g for g in range(2) if not is_scalar(b, t, g)]
+            if not cols:
+                return
+            n = len(cols)
+            if i == 0:
+                xg_t[j] = sb("xg", [P, 2 * 2 * P * 4], BF16, bufs=3, pool=work)
+            bk = tp_bank()
+            words = xs_t[j, i][:].bitcast(F32)
+            for s, g in enumerate(cols):
+                for u in range(2):
+                    at = (2 * s + u) * P
+                    nc.tensor.transpose(bk[:, at : at + P], words[:, 256 * g + u : 256 * (g + 1) : 2], ident[:])
+            nc.scalar.copy(
+                out=xg_t[j][:].bitcast(F32)[:, i * n * 256 : (i + 1) * n * 256].rearrange("p (g r u) -> p g r u", g=n, u=2),
+                in_=bk[:, 0 : n * 256].rearrange("p (g u r) -> p g r u", g=n, u=2),
+            )
 
-        def x_quant(j, parts=1):
-            codes = sb("xq", [P, 512], U32, bufs=3, pool=work)
-            scales = sb("xq_s", [P, 512], U8, bufs=3, pool=work)
-            n = 512 // parts
-            for i in range(parts):
-                quantize(codes[:, i * n : (i + 1) * n], scales[:, i * n : (i + 1) * n], xg_t[j][:, 4 * i * n : 4 * (i + 1) * n])
-            xq_t[j] = (codes, scales)
+        def x_quant(j, i0=0, i1=2):
+            b, t, h0 = where(j)
+            n = len([g for g in range(2) if not is_scalar(b, t, g)]) * P
+            if n == 0:
+                return
+            if i0 == 0:
+                xq_t[j] = (sb("xq", [P, 512], U32, bufs=3, pool=work), sb("xq_s", [P, 512], U8, bufs=3, pool=work))
+            codes, scales = xq_t[j]
+            quantize(codes[:, i0 * n : i1 * n], scales[:, i0 * n : i1 * n], xg_t[j][:, 4 * i0 * n : 4 * i1 * n])
+
+        fc_t = {}
+        fb_t = {}
+        fp_t = {}
+        fg_t = {}
+        fq_t = {}
+
+        def f_cast(b, t, g, h):
+            if h == 0:
+                fc_t[b, t, g] = sb("fc", [P, HI, 512], BF16, bufs=1, pool=work)
+            nc.scalar.copy(out=fc_t[b, t, g][:, h, :], in_=xb[b][t][:, h, g * 512 : (g + 1) * 512].bitcast(FP8))
+
+        def f_turn(b, t, g, v):
+            bk = psum.tile([P, 1024], BF16, name="tp", tag="tp", bufs=3)
+            for s in range(2):
+                for h in range(HI):
+                    at = s * 512 + h * P
+                    nc.tensor.transpose(bk[:, at : at + P], fc_t[b, t, g][:, h, 2 * v + s : 512 : 4], ident_b[:])
+            fb_t[b, t, g, v] = bk
+
+        def f_scale(b, t, g, k):
+            if k == 0:
+                fp_t[b, t, g] = sb("fp", [P, 4, 512], BF16, bufs=1, pool=work)
+            nc.scalar.activation(
+                out=fp_t[b, t, g][:, k, :],
+                in_=fb_t[b, t, g, k // 2][:, (k % 2) * 512 : (k % 2 + 1) * 512],
+                func=ACT.Copy,
+                scale=scol[:, g, k : k + 1],
+            )
+
+        def f_mix(b, t, g, n):
+            if n == 0:
+                fg_t[b, t, g] = sb("fg", [P, 2048], BF16, bufs=2, pool=work)
+            rows = slice(n * 256, (n + 1) * 256)
+            nc.scalar.copy(
+                out=fg_t[b, t, g][:, n * 1024 : (n + 1) * 1024].rearrange("p (r k) -> p r k", k=4),
+                in_=fp_t[b, t, g][:, :, rows].rearrange("p k r -> p r k"),
+            )
+
+        def f_quant(b, t, g):
+            codes, scales = sb("fq", [P, 512], U32, bufs=2, pool=work), sb("fq_s", [P, 512], U8, bufs=2, pool=work)
+            quantize(codes[:], scales[:], fg_t[b, t, g][:])
+            fq_t[b, t, g] = (codes, scales)
 
         def mm1(j):
             b, t, h0 = where(j)
-            codes, scales = xq_t[j]
+            cols = [g for g in range(2) if not is_scalar(b, t, g)]
             ys = []
             for i in range(2):
                 y = bank("y", 2)
                 for g in range(2):
-                    sl = slice((2 * i + g) * P, (2 * i + g + 1) * P)
+                    if g in cols:
+                        codes, scales = xq_t[j]
+                        at = (len(cols) * i + cols.index(g)) * P
+                    else:
+                        codes, scales = fq_t[b, t, g]
+                        at = (h0 + i) * P
+                    sl = slice(at, at + P)
                     ocols = slice(g * NO, (g + 1) * NO)
                     mx(y[:], codes[:, sl], scales[:, sl], wq[:, ocols], wq_s[:, ocols], start=g == 0, stop=g == 1)
                 ys.append(y)
@@ -317,76 +479,89 @@ def tile_matrixvtringraybev_kernel(tc, x_bytes, x_scale, wc, gw, dl, gd, ring, r
                 nc.scalar.copy(out=m[:], in_=ys[0][:])
                 m_t[b, t] = m
 
-        def y_max(j, eng="s"):
+        def max_a(j):
+            b, t, h0 = where(j)
+            if h0 == 2:
+                nc.vector.tensor_tensor(out=m_t[b, t][:], in0=y_t[j][0][:], in1=m_t[b, t][:], op=ALU.max)
+
+        def max_b(j):
             b, t, h0 = where(j)
             m = m_t[b, t]
-            ys = y_t[j]
+            y = y_t[j][1]
             if h0 == 0:
-                nc.vector.tensor_tensor(out=m[:], in0=ys[1][:], in1=m[:], op=ALU.max)
+                nc.vector.tensor_tensor(out=m[:], in0=y[:], in1=m[:], op=ALU.max)
             else:
-                nc.vector.tensor_tensor(out=m[:], in0=ys[0][:], in1=m[:], op=ALU.max)
                 nc.vector.scalar_tensor_tensor(
-                    out=m[:], in0=ys[1][:], scalar=1.0, in1=m[:], op0=ALU.mult, op1=ALU.max, accum_out=msum[b][t][:]
+                    out=m[:], in0=y[:], scalar=1.0, in1=m[:], op0=ALU.mult, op1=ALU.max, accum_out=msum[b][t][:]
                 )
-                centre(b, t, eng)
 
-        pre = {
-            1: [(wc_quant, 0), (wc_quant, 1)],
-            2: [(ring_turn, 0), (ring_turn, 1)],
-            3: [(d_turn, 0, 0), (d_turn, 0, 1), (ring_turn, 2), (ring_turn, 3)],
-            4: [(ray_turn, 0), (ray_turn, 1), (d_quant, 0)],
-            5: [(ray_turn, 2), (ray_turn, 3)],
-            7: [(d_turn, 1, 0), (d_turn, 1, 1)],
-        }
-        post = {
-            0: [(dmax, 0)],
-            1: [(dexp, 0)],
-            2: [(drecip, 0), (dprod, 0, 0), (dprod, 0, 1), (dprod, 0, 2), (dprod, 0, 3)],
-            3: [(ring_quant, 0), (dmax, 1)],
-            4: [(ring_quant, 1), (mm2, 0, 0), (mm2, 0, 1), (dexp, 1)],
-            5: [(tm, 0, 0), (tm, 0, 1), (mm2, 0, 2), (mm2, 0, 3), (drecip, 1), (dprod, 1, 0), (dprod, 1, 1)],
-            6: [(tm, 0, 2), (tm, 0, 3), (mm2, 0, 4), (mm2, 0, 5), (dprod, 1, 2), (dprod, 1, 3)],
-            7: [(tm, 0, 4), (tm, 0, 5), (mm2, 0, 6), (mm2, 0, 7), (tm_quant, 0, 0)],
-            8: [(tm, 0, 6), (tm, 0, 7), (d_quant, 1), (mm2, 1, 0), (mm2, 1, 1)],
-            9: [(tm_quant, 0, 1), (tm, 1, 0), (tm, 1, 1), (mm2, 1, 2), (mm2, 1, 3), (ctx_interleave, 0, 0, "s"), (ctx_interleave, 0, 1, "s")],
-            10: [(tm, 1, 2), (tm, 1, 3), (mm2, 1, 4), (mm2, 1, 5), (ctx_quant, 0, 0), (ctx_quant, 0, 1)],
-            11: [(tm, 1, 4), (tm, 1, 5), (mm2, 1, 6), (mm2, 1, 7), (tm_quant, 1, 0)],
-            12: [(tm, 1, 6), (tm, 1, 7)],
-            13: [(tm_quant, 1, 1)],
-        }
+        def mean_b(j, eng="s"):
+            b, t, h0 = where(j)
+            if h0 == 2:
+                negmean(b, t)
+                centre(b, t, eng)
 
         def run(items):
             for item in items:
                 item[0](*item[1:])
 
-        def mm3_step(j):
-            if 12 <= j < 16:
-                for c in (2 * (j - 12), 2 * (j - 12) + 1):
-                    mm3(0, c, "s", o_bank())
+        def ctx_il_s(b, i):
+            ctx_interleave(b, i, "s")
+
+        def mm3_s(b, c):
+            mm3(b, c, "s", r_bank())
+
+        def mean_item(b, t):
+            negmean(b, t)
+
+        def centre_item(b, t):
+            centre(b, t, "s")
+
+        FN = {
+            "dmax": dmax, "ringq": ring_quant, "recip": drecip, "dprod": dprod, "dq": d_quant, "tm": tm, "tmq": tm_quant,
+            "fq": f_quant, "cq": ctx_quant, "wq": wc_quant, "mm2": mm2, "ring": ring_turn, "ray": ray_turn, "exp": dexp,
+            "dt": d_turn, "fc": f_cast, "ft": f_turn, "fs": f_scale, "fm": f_mix, "ci": ctx_il_s, "mm3": mm3_s, "wi": wc_interleave,
+            "mean": mean_item, "centre": centre_item,
+        }
+
+        def at(j, p):
+            for item in PLAN.get((j, p), []):
+                FN[item[0]](*item[1:])
 
         n_pairs = 16
-        for j in range(n_pairs):
-            if j == 0:
-                wc_interleave(0)
-                wc_interleave(1)
-            x_mult(j)
+        for j in range(18):
+            x = j < n_pairs
+            if j == 2:
+                load_ray()
+            at(j, 0)
+            if x:
+                x_mult(j, 0)
+            at(j, 1)
             if j >= 2:
-                y_max(j - 2)
-            if j >= 1:
+                max_a(j - 2)
+            if x:
+                x_mult(j, 1)
+            if 1 <= j <= 16:
                 x_quant(j - 1)
-            x_turn(j)
-            run(pre.get(j, []))
-            if j >= 1:
+            if x:
+                x_turn(j, 0)
+            at(j, 2)
+            if x:
+                x_turn(j, 1)
+            at(j, 3)
+            if j >= 2:
+                max_b(j - 2)
+            if 1 <= j <= 16:
                 mm1(j - 1)
-            run(post.get(j, []))
-            mm3_step(j)
-        y_max(n_pairs - 2)
-        x_quant(n_pairs - 1, parts=2)
-        mm1(n_pairs - 1)
-        y_max(n_pairs - 1, "v")
+            at(j, 4)
+        mean_b(n_pairs - 1, "v")
+        at(18, 0)
         ctx_interleave(1, 0, "v")
         ctx_interleave(1, 1, "s")
+        at(18, 1)
         ctx_quant(1, 0)
         ctx_quant(1, 1)
+        at(18, 2)
         for c in range(8):
-            mm3(1, c, "sv"[c % 2], o_bank() if c % 2 else tp_bank())
+            at(19 + c, 0)
+            mm3(1, c, EV[c], (tp_bank, r_bank, tp_bank, y_bank)[c % 4]())

@@ -19,75 +19,77 @@ P = 128
 BY_SCALAR = [(1, 1, 0), (1, 3, 0)]
 PLAN = {
     (0, 0): [('wi', 0)],
-    (0, 4): [('wi', 1)],
-    (1, 2): [('dmax', 0), ('wq', 0)],
-    (1, 3): [('dmax', 1), ('wq', 1)],
-    (1, 4): [('dmax', 2)],
-    (2, 0): [('ring', 3)],
-    (2, 1): [('dmax', 3)],
-    (2, 2): [('dmax', 4), ('ring', 2)],
-    (2, 4): [('dmax', 5)],
-    (3, 0): [('exp', 0, 2), ('exp', 0, 3)],
-    (3, 2): [('exp', 0, 1), ('ring', 1)],
-    (3, 3): [('exp', 0, 0)],
-    (4, 0): [('fc', 1, 1, 0, 0)],
-    (4, 1): [('ray', 0), ('ring', 0)],
-    (4, 3): [('fc', 1, 1, 0, 1), ('recip', 0)],
-    (4, 4): [('dprod', 0, 3)],
-    (5, 0): [('fc', 1, 1, 0, 3), ('dprod', 0, 0), ('dprod', 0, 1)],
-    (5, 1): [('dprod', 0, 2), ('dt', 0, 0)],
-    (5, 2): [('ray', 1), ('fc', 1, 1, 0, 2), ('ringq', 1)],
-    (5, 4): [('dt', 0, 1)],
-    (6, 2): [('ft', 1, 1, 0, 0), ('dq', 0), ('exp', 1, 3)],
-    (6, 3): [('fs', 1, 1, 0, 0), ('exp', 1, 2), ('exp', 1, 1)],
-    (6, 4): [('fs', 1, 1, 0, 1), ('mean', 0, 1)],
-    (7, 1): [('ft', 1, 1, 0, 1), ('exp', 1, 0)],
-    (7, 2): [('fs', 1, 1, 0, 2)],
-    (7, 3): [('fc', 1, 3, 0, 0), ('ringq', 0), ('mm2', 0, 0), ('recip', 1)],
-    (7, 4): [('fs', 1, 1, 0, 3), ('centre', 0, 1), ('dprod', 1, 0), ('mean', 0, 0), ('ray', 2)],
-    (8, 0): [('centre', 0, 0), ('dprod', 1, 1)],
-    (8, 2): [('fm', 1, 1, 0, 0), ('mean', 0, 2)],
-    (8, 3): [('mm2', 0, 1), ('fc', 1, 3, 0, 3)],
-    (8, 4): [('dt', 1, 0)],
-    (9, 1): [('tm', 0, 0)],
-    (9, 2): [('fc', 1, 3, 0, 2)],
-    (9, 3): [('dprod', 1, 3), ('fm', 1, 1, 0, 1)],
-    (9, 4): [('ray', 3), ('tm', 0, 1)],
-    (10, 1): [('mm2', 0, 2)],
-    (10, 2): [('fc', 1, 3, 0, 1), ('dprod', 1, 2)],
-    (10, 4): [('ft', 1, 3, 0, 0), ('fq', 1, 1, 0), ('centre', 0, 2), ('fs', 1, 3, 0, 0)],
-    (11, 0): [('fs', 1, 3, 0, 1)],
-    (11, 1): [('dt', 1, 1), ('mean', 0, 3)],
-    (11, 2): [('ft', 1, 3, 0, 1), ('tmq', 0, 0), ('fs', 1, 3, 0, 3)],
-    (11, 3): [('centre', 0, 3), ('fs', 1, 3, 0, 2)],
-    (11, 4): [('ci', 0, 1), ('mm2', 0, 3)],
-    (12, 1): [('tm', 0, 2), ('dq', 1)],
-    (12, 2): [('mm2', 0, 4), ('tm', 0, 3), ('ci', 0, 0)],
-    (12, 4): [('tm', 0, 4), ('tmq', 0, 1), ('mean', 1, 0)],
-    (13, 0): [('cq', 0, 1), ('mm2', 0, 5)],
-    (13, 1): [('centre', 1, 0), ('fm', 1, 3, 0, 0), ('cq', 0, 0)],
-    (13, 2): [('mm3', 0, 0)],
-    (13, 4): [('fm', 1, 3, 0, 1)],
-    (14, 1): [('mm2', 0, 7)],
-    (14, 2): [('mm3', 0, 3), ('tm', 0, 5)],
-    (14, 3): [('mm2', 0, 6)],
-    (14, 4): [('tm', 0, 7)],
-    (15, 0): [('mm3', 0, 2)],
-    (15, 3): [('fq', 1, 3, 0), ('mm3', 0, 1)],
-    (15, 4): [('tm', 0, 6), ('mm2', 1, 1)],
-    (16, 1): [('tmq', 0, 2), ('mm2', 1, 0), ('tmq', 0, 3)],
-    (16, 2): [('mean', 1, 1), ('mm3', 0, 7), ('mean', 1, 2)],
-    (16, 4): [('mm3', 0, 5), ('tm', 1, 0)],
-    (17, 0): [('tm', 1, 1)],
-    (17, 1): [('centre', 1, 2)],
-    (17, 2): [('centre', 1, 1), ('mm2', 1, 3)],
-    (17, 3): [('mm2', 1, 2), ('tmq', 1, 0)],
-    (17, 4): [('tm', 1, 2)],
-    (18, 0): [('mm3', 0, 4), ('tm', 1, 3)],
-    (18, 1): [('mm2', 1, 4), ('tm', 1, 4)],
-    (18, 2): [('mm3', 0, 6), ('mm2', 1, 5)],
-    (19, 0): [('tm', 1, 5), ('mm2', 1, 6)],
-    (20, 0): [('tmq', 1, 1), ('tmq', 1, 2), ('mm2', 1, 7), ('tm', 1, 7), ('tm', 1, 6)],
+    (0, 3): [('wi', 1)],
+    (1, 2): [('dmax', 0), ('dmax', 1), ('dmax', 2), ('wq', 0), ('wq', 1)],
+    (1, 3): [('dmax', 3)],
+    (2, 0): [('ring', 2)],
+    (2, 1): [('dmax', 4)],
+    (2, 2): [('dmax', 5), ('exp', 0, 2)],
+    (2, 3): [('exp', 0, 0), ('exp', 0, 1)],
+    (2, 4): [('exp', 0, 3)],
+    (3, 0): [('fc', 1, 1, 0, 0), ('ring', 0)],
+    (3, 2): [('fc', 1, 1, 0, 2)],
+    (3, 3): [('recip', 0)],
+    (3, 4): [('dprod', 0, 2)],
+    (4, 0): [('exp', 1, 2)],
+    (4, 1): [('ring', 3)],
+    (4, 2): [('dprod', 0, 1)],
+    (4, 3): [('dprod', 0, 0), ('ray', 2), ('fc', 1, 1, 0, 3)],
+    (4, 4): [('ring', 1), ('exp', 1, 3)],
+    (5, 0): [('dt', 0, 0)],
+    (5, 1): [('exp', 1, 0)],
+    (5, 2): [('fc', 1, 1, 0, 1), ('dprod', 0, 3)],
+    (5, 3): [('ringq', 0), ('exp', 1, 1)],
+    (5, 4): [('ft', 1, 1, 0, 0)],
+    (6, 1): [('fs', 1, 1, 0, 0), ('fs', 1, 1, 0, 1)],
+    (6, 2): [('dt', 0, 1), ('mean', 0, 1)],
+    (6, 3): [('recip', 1)],
+    (6, 4): [('dprod', 1, 2), ('ray', 0), ('dprod', 1, 3), ('mean', 0, 0)],
+    (7, 0): [('ft', 1, 1, 0, 1), ('dprod', 1, 0), ('fs', 1, 1, 0, 2)],
+    (7, 1): [('fs', 1, 1, 0, 3)],
+    (7, 2): [('dq', 0), ('ringq', 1), ('fm', 1, 1, 0, 0)],
+    (7, 4): [('mm2', 0, 0), ('fm', 1, 1, 0, 1)],
+    (8, 0): [('ray', 1)],
+    (8, 1): [('centre', 0, 1)],
+    (8, 2): [('mean', 0, 2), ('fc', 1, 3, 0, 0), ('dprod', 1, 1), ('tm', 0, 0)],
+    (8, 4): [('ray', 3), ('mm2', 0, 2), ('dt', 1, 0)],
+    (9, 1): [('centre', 0, 0), ('mm2', 0, 1)],
+    (9, 2): [('fc', 1, 3, 0, 3)],
+    (10, 0): [('fc', 1, 3, 0, 1), ('fc', 1, 3, 0, 2)],
+    (10, 1): [('dt', 1, 1), ('tm', 0, 2), ('tm', 0, 1), ('mean', 0, 3)],
+    (10, 2): [('centre', 0, 3)],
+    (10, 3): [('mm2', 0, 3)],
+    (11, 0): [('centre', 0, 2)],
+    (11, 1): [('tm', 0, 3), ('dq', 1), ('fq', 1, 1, 0), ('ci', 0, 0)],
+    (11, 2): [('ft', 1, 3, 0, 1), ('ft', 1, 3, 0, 0), ('fs', 1, 3, 0, 0), ('fs', 1, 3, 0, 2), ('tmq', 0, 1)],
+    (11, 3): [('fs', 1, 3, 0, 3)],
+    (11, 4): [('ci', 0, 1), ('mm2', 0, 4)],
+    (12, 1): [('fs', 1, 3, 0, 1), ('cq', 0, 0)],
+    (12, 3): [('mean', 1, 0)],
+    (12, 4): [('mm2', 0, 7), ('fm', 1, 3, 0, 0)],
+    (13, 0): [('tm', 0, 4), ('cq', 0, 1), ('fm', 1, 3, 0, 1), ('tmq', 0, 0)],
+    (13, 1): [('mm3', 0, 3)],
+    (13, 2): [('mm2', 0, 5)],
+    (14, 1): [('tm', 0, 7)],
+    (14, 4): [('mm3', 0, 1), ('tm', 0, 5), ('fq', 1, 3, 0)],
+    (15, 1): [('mm2', 1, 0), ('mm2', 0, 6), ('mm3', 0, 0)],
+    (15, 4): [('tm', 0, 6), ('tm', 1, 0), ('mm3', 0, 2)],
+    (16, 0): [('mm2', 1, 1), ('tmq', 0, 3)],
+    (16, 1): [('tmq', 0, 2)],
+    (16, 2): [('mean', 1, 2), ('centre', 1, 0), ('mean', 1, 1)],
+    (16, 3): [('mm3', 0, 7), ('centre', 1, 2)],
+    (16, 4): [('mm3', 0, 5), ('centre', 1, 1)],
+    (17, 0): [('tm', 1, 1), ('mm2', 1, 2)],
+    (17, 1): [('mm2', 1, 3)],
+    (17, 2): [('tmq', 1, 0)],
+    (17, 3): [('mm3', 0, 4)],
+    (17, 4): [('mm2', 1, 4)],
+    (18, 0): [('tm', 1, 2)],
+    (18, 1): [('tm', 1, 3)],
+    (18, 2): [('tmq', 1, 1), ('mm3', 0, 6), ('mm2', 1, 7)],
+    (19, 0): [('mm2', 1, 5)],
+    (20, 0): [('tm', 1, 4), ('mm2', 1, 6), ('tm', 1, 5), ('tm', 1, 6)],
+    (21, 0): [('tmq', 1, 2), ('tm', 1, 7)],
     (25, 0): [('tmq', 1, 3)],
 }
 EV = "sssssssv"
@@ -306,7 +308,7 @@ def tile_matrixvtringraybev_kernel(tc, x_bytes, x_scale, wc, gw, dl, gd, ring, r
             turn_pair([half[:, c, :], half[:, c + 1, :]], rayg[:, i * 1024 : (i + 1) * 1024])
 
         def mm2(b, c):
-            o = o_bank()
+            o = y_bank() if (b, c) in ((1, 4), (1, 5)) else o_bank()
             for t in range(4):
                 sl = slice(t * P, (t + 1) * P)
                 cs = slice(c * P, (c + 1) * P)
@@ -456,11 +458,11 @@ def tile_matrixvtringraybev_kernel(tc, x_bytes, x_scale, wc, gw, dl, gd, ring, r
             quantize(codes[:], scales[:], fg_t[b, t, g][:])
             fq_t[b, t, g] = (codes, scales)
 
-        def mm1(j):
+        def mm1(j, i0=0, i1=2):
             b, t, h0 = where(j)
             cols = [g for g in range(2) if not is_scalar(b, t, g)]
-            ys = []
-            for i in range(2):
+            ys = y_t.setdefault(j, [])
+            for i in range(i0, i1):
                 y = bank("y", 2)
                 for g in range(2):
                     if g in cols:
@@ -473,8 +475,7 @@ def tile_matrixvtringraybev_kernel(tc, x_bytes, x_scale, wc, gw, dl, gd, ring, r
                     ocols = slice(g * NO, (g + 1) * NO)
                     mx(y[:], codes[:, sl], scales[:, sl], wq[:, ocols], wq_s[:, ocols], start=g == 0, stop=g == 1)
                 ys.append(y)
-            y_t[j] = ys
-            if h0 == 0:
+            if h0 == 0 and i0 == 0:
                 m = sb("m", [P, NO], F32, bufs=4, pool=work)
                 nc.scalar.copy(out=m[:], in_=ys[0][:])
                 m_t[b, t] = m
@@ -541,8 +542,10 @@ def tile_matrixvtringraybev_kernel(tc, x_bytes, x_scale, wc, gw, dl, gd, ring, r
                 max_a(j - 2)
             if x:
                 x_mult(j, 1)
-            if 1 <= j <= 16:
+            if 1 <= j < 16:
                 x_quant(j - 1)
+            elif j == 16:
+                x_quant(15, 0, 1)
             if x:
                 x_turn(j, 0)
             at(j, 2)
@@ -551,8 +554,12 @@ def tile_matrixvtringraybev_kernel(tc, x_bytes, x_scale, wc, gw, dl, gd, ring, r
             at(j, 3)
             if j >= 2:
                 max_b(j - 2)
-            if 1 <= j <= 16:
+            if 1 <= j < 16:
                 mm1(j - 1)
+            elif j == 16:
+                mm1(15, 0, 1)
+                x_quant(15, 1, 2)
+                mm1(15, 1, 2)
             at(j, 4)
         mean_b(n_pairs - 1, "v")
         at(18, 0)
@@ -564,4 +571,4 @@ def tile_matrixvtringraybev_kernel(tc, x_bytes, x_scale, wc, gw, dl, gd, ring, r
         at(18, 2)
         for c in range(8):
             at(19 + c, 0)
-            mm3(1, c, EV[c], (tp_bank, r_bank, tp_bank, y_bank)[c % 4]())
+            mm3(1, c, EV[c], (tp_bank, tp_bank, r_bank)[c % 3]())

@@ -13,88 +13,104 @@ ACT = mybir.ActivationFunctionType
 ALU = mybir.AluOpType
 AXIS = mybir.AxisListType
 
-B, HI, W, C, ND, NP, NO = 2, 4, 512, 1024, 512, 1024, 512
 P = 128
+PACK = 4
+PASS = P * PACK
+B = 2
+HEIGHTS = 4
+W = 512
+C = 1024
+ND = 512
+CELLS = 1024
+CHUNKS = CELLS // P
+NO = 512
+PAIRS = B * PACK * HEIGHTS // 2
 
-BY_SCALAR = [(1, 1, 0), (1, 3, 0)]
-PLAN = {
-    (0, 0): [('wi', 0)],
-    (0, 3): [('wi', 1)],
-    (1, 2): [('dmax', 0), ('dmax', 1), ('dmax', 2), ('wq', 0), ('wq', 1)],
-    (1, 3): [('dmax', 3)],
-    (2, 0): [('ring', 2)],
-    (2, 1): [('dmax', 4)],
-    (2, 2): [('dmax', 5), ('exp', 0, 2)],
-    (2, 3): [('exp', 0, 0), ('exp', 0, 1)],
-    (2, 4): [('exp', 0, 3)],
-    (3, 0): [('fc', 1, 1, 0, 0), ('ring', 0)],
-    (3, 2): [('fc', 1, 1, 0, 2)],
-    (3, 3): [('recip', 0)],
-    (3, 4): [('dprod', 0, 2)],
-    (4, 0): [('exp', 1, 2)],
-    (4, 1): [('ring', 3)],
-    (4, 2): [('dprod', 0, 1)],
-    (4, 3): [('dprod', 0, 0), ('ray', 2), ('fc', 1, 1, 0, 3)],
-    (4, 4): [('ring', 1), ('exp', 1, 3)],
-    (5, 0): [('dt', 0, 0)],
-    (5, 1): [('exp', 1, 0)],
-    (5, 2): [('fc', 1, 1, 0, 1), ('dprod', 0, 3)],
-    (5, 3): [('ringq', 0), ('exp', 1, 1)],
-    (5, 4): [('ft', 1, 1, 0, 0)],
-    (6, 1): [('fs', 1, 1, 0, 0), ('fs', 1, 1, 0, 1)],
-    (6, 2): [('dt', 0, 1), ('mean', 0, 1)],
-    (6, 3): [('recip', 1)],
-    (6, 4): [('dprod', 1, 2), ('ray', 0), ('dprod', 1, 3), ('mean', 0, 0)],
-    (7, 0): [('ft', 1, 1, 0, 1), ('dprod', 1, 0), ('fs', 1, 1, 0, 2)],
-    (7, 1): [('fs', 1, 1, 0, 3)],
-    (7, 2): [('dq', 0), ('ringq', 1), ('fm', 1, 1, 0, 0)],
-    (7, 4): [('mm2', 0, 0), ('fm', 1, 1, 0, 1)],
-    (8, 0): [('ray', 1)],
-    (8, 1): [('centre', 0, 1)],
-    (8, 2): [('mean', 0, 2), ('fc', 1, 3, 0, 0), ('dprod', 1, 1), ('tm', 0, 0)],
-    (8, 4): [('ray', 3), ('mm2', 0, 2), ('dt', 1, 0)],
-    (9, 1): [('centre', 0, 0), ('mm2', 0, 1)],
-    (9, 2): [('fc', 1, 3, 0, 3)],
-    (10, 0): [('fc', 1, 3, 0, 1), ('fc', 1, 3, 0, 2)],
-    (10, 1): [('dt', 1, 1), ('tm', 0, 2), ('tm', 0, 1), ('mean', 0, 3)],
-    (10, 2): [('centre', 0, 3)],
-    (10, 3): [('mm2', 0, 3)],
-    (11, 0): [('centre', 0, 2)],
-    (11, 1): [('tm', 0, 3), ('dq', 1), ('fq', 1, 1, 0), ('ci', 0, 0)],
-    (11, 2): [('ft', 1, 3, 0, 1), ('ft', 1, 3, 0, 0), ('fs', 1, 3, 0, 0), ('fs', 1, 3, 0, 2), ('tmq', 0, 1)],
-    (11, 3): [('fs', 1, 3, 0, 3)],
-    (11, 4): [('ci', 0, 1), ('mm2', 0, 4)],
-    (12, 1): [('fs', 1, 3, 0, 1), ('cq', 0, 0)],
-    (12, 3): [('mean', 1, 0)],
-    (12, 4): [('mm2', 0, 7), ('fm', 1, 3, 0, 0)],
-    (13, 0): [('tm', 0, 4), ('cq', 0, 1), ('fm', 1, 3, 0, 1), ('tmq', 0, 0)],
-    (13, 1): [('mm3', 0, 3)],
-    (13, 2): [('mm2', 0, 5)],
-    (14, 1): [('tm', 0, 7)],
-    (14, 4): [('mm3', 0, 1), ('tm', 0, 5), ('fq', 1, 3, 0)],
-    (15, 1): [('mm2', 1, 0), ('mm2', 0, 6), ('mm3', 0, 0)],
-    (15, 4): [('tm', 0, 6), ('tm', 1, 0), ('mm3', 0, 2)],
-    (16, 0): [('mm2', 1, 1), ('tmq', 0, 3)],
-    (16, 1): [('tmq', 0, 2)],
-    (16, 2): [('mean', 1, 2), ('centre', 1, 0), ('mean', 1, 1)],
-    (16, 3): [('mm3', 0, 7), ('centre', 1, 2)],
-    (16, 4): [('mm3', 0, 5), ('centre', 1, 1)],
-    (17, 0): [('tm', 1, 1), ('mm2', 1, 2)],
-    (17, 1): [('mm2', 1, 3)],
-    (17, 2): [('tmq', 1, 0)],
-    (17, 3): [('mm3', 0, 4)],
-    (17, 4): [('mm2', 1, 4)],
-    (18, 0): [('tm', 1, 2)],
-    (18, 1): [('tm', 1, 3)],
-    (18, 2): [('tmq', 1, 1), ('mm3', 0, 6), ('mm2', 1, 7)],
-    (19, 0): [('mm2', 1, 5)],
-    (20, 0): [('tm', 1, 4), ('mm2', 1, 6), ('tm', 1, 5), ('tm', 1, 6)],
-    (21, 0): [('tmq', 1, 2), ('tm', 1, 7)],
-    (25, 0): [('tmq', 1, 3)],
+BY_SCALAR = ((1, 1, 0), (1, 3, 0),)
+
+OTHER_WORK = {
+    (0, 0): [("wc_mix", 0)],
+    (0, 4): [("gd_spread",)],
+    (1, 1): [("wc_mix", 1)],
+    (1, 2): [("dl_max", 0), ("dl_max", 1), ("wc_quant", 0), ("dl_max", 2), ("wc_quant", 1)],
+    (1, 3): [("dl_max", 3)],
+    (1, 4): [("ring_turn", 2)],
+    (2, 1): [("dl_max", 4)],
+    (2, 2): [("dl_max", 5)],
+    (2, 3): [("dl_exp", 0, 3)],
+    (2, 4): [("dl_exp", 0, 1)],
+    (3, 0): [("dl_exp", 0, 2), ("dl_exp", 0, 0)],
+    (3, 1): [("ring_turn", 3)],
+    (3, 2): [("d_inv", 0), ("ring_turn", 0)],
+    (3, 3): [("f_cast", 1, 1, 0, 0), ("f_cast", 1, 1, 0, 2)],
+    (3, 4): [("ray_turn", 2), ("d_prod", 0, 0)],
+    (4, 2): [("f_cast", 1, 1, 0, 3)],
+    (4, 3): [("d_prod", 0, 3), ("dl_exp", 1, 1), ("d_prod", 0, 1)],
+    (5, 0): [("ring_turn", 1), ("f_cast", 1, 1, 0, 1)],
+    (5, 1): [("d_turn", 0, 0)],
+    (5, 3): [("d_prod", 0, 2), ("dl_exp", 1, 3), ("ring_quant", 1)],
+    (5, 4): [("ring_quant", 0), ("dl_exp", 1, 0), ("dl_exp", 1, 2)],
+    (6, 0): [("f_turn", 1, 1, 0, 0), ("f_scale", 1, 1, 0, 0), ("f_scale", 1, 1, 0, 1)],
+    (6, 1): [("ctx_shift", 0, 1)],
+    (6, 2): [("d_turn", 0, 1)],
+    (6, 3): [("ctx_centre", 0, 1), ("d_inv", 1)],
+    (6, 4): [("d_prod", 1, 3), ("f_turn", 1, 1, 0, 1)],
+    (7, 0): [("f_scale", 1, 1, 0, 2)],
+    (7, 1): [("d_prod", 1, 0), ("d_prod", 1, 1), ("f_cast", 1, 3, 0, 0), ("f_scale", 1, 1, 0, 3)],
+    (7, 2): [("ray_turn", 0), ("ctx_shift", 0, 0)],
+    (7, 3): [("d_prod", 1, 2)],
+    (7, 4): [("d_quant", 0), ("rd_mm", 0, 0)],
+    (8, 0): [("f_mix", 1, 1, 0, 0), ("f_cast", 1, 3, 0, 3)],
+    (8, 2): [("ray_turn", 1)],
+    (8, 3): [("tm_prod", 0, 0)],
+    (8, 4): [("f_mix", 1, 1, 0, 1), ("ctx_centre", 0, 0), ("d_turn", 1, 0), ("rd_mm", 0, 2)],
+    (9, 1): [("rd_mm", 0, 1), ("ctx_shift", 0, 2), ("d_turn", 1, 1)],
+    (9, 2): [("f_quant", 1, 1, 0)],
+    (9, 4): [("tm_prod", 0, 2), ("ctx_shift", 0, 3)],
+    (10, 0): [("ctx_centre", 0, 3), ("ray_turn", 3), ("tm_prod", 0, 1)],
+    (10, 2): [("ctx_centre", 0, 2), ("f_cast", 1, 3, 0, 1), ("rd_mm", 0, 3)],
+    (10, 3): [("d_quant", 1)],
+    (10, 4): [("f_cast", 1, 3, 0, 2), ("rd_mm", 0, 4)],
+    (11, 0): [("ctx_mix", 0, 0)],
+    (11, 1): [("tm_prod", 0, 3)],
+    (11, 2): [
+        ("tm_quant", 0, 1), ("tm_prod", 0, 4), ("ctx_mix", 0, 1), ("f_turn", 1, 3, 0, 1), ("f_turn", 1, 3, 0, 0),
+        ("f_scale", 1, 3, 0, 0), ("f_scale", 1, 3, 0, 2),
+    ],
+    (11, 3): [("f_scale", 1, 3, 0, 3)],
+    (12, 0): [("ctx_quant", 0, 0), ("f_scale", 1, 3, 0, 1), ("tm_quant", 0, 0)],
+    (12, 1): [("ctx_shift", 1, 0), ("rd_mm", 0, 7), ("ctx_quant", 0, 1)],
+    (12, 2): [("f_mix", 1, 3, 0, 0)],
+    (13, 0): [("f_mix", 1, 3, 0, 1)],
+    (13, 1): [("out_mm", 0, 0)],
+    (13, 2): [("tm_prod", 0, 7)],
+    (13, 4): [("rd_mm", 0, 5)],
+    (14, 0): [("rd_mm", 0, 6)],
+    (14, 1): [("out_mm", 0, 1)],
+    (14, 3): [("ctx_centre", 1, 0)],
+    (14, 4): [("f_quant", 1, 3, 0)],
+    (15, 0): [("tm_prod", 0, 5), ("rd_mm", 1, 0)],
+    (15, 1): [("out_mm", 0, 3)],
+    (15, 3): [("out_mm", 0, 2)],
+    (15, 4): [("tm_prod", 0, 6), ("rd_mm", 1, 1)],
+    (16, 0): [("tm_quant", 0, 2), ("tm_quant", 0, 3)],
+    (16, 1): [("ctx_shift", 1, 2)],
+    (16, 2): [("ctx_centre", 1, 2), ("tm_prod", 1, 0), ("out_mm", 0, 7)],
+    (16, 4): [("ctx_shift", 1, 1), ("ctx_centre", 1, 1), ("out_mm", 0, 5)],
+    (17, 0): [("rd_mm", 1, 2)],
+    (17, 2): [("tm_prod", 1, 1), ("out_mm", 0, 4)],
+    (17, 3): [("rd_mm", 1, 3)],
+    (17, 4): [("rd_mm", 1, 5), ("tm_prod", 1, 2), ("rd_mm", 1, 4)],
+    (18, 0): [("tm_prod", 1, 3)],
+    (18, 1): [("tm_quant", 1, 0)],
+    (18, 2): [("out_mm", 0, 6), ("tm_quant", 1, 1), ("tm_prod", 1, 4)],
+    (19, 0): [("tm_prod", 1, 5), ("rd_mm", 1, 7)],
+    (20, 0): [("tm_prod", 1, 7)],
+    (21, 0): [("rd_mm", 1, 6), ("tm_quant", 1, 2), ("tm_prod", 1, 6)],
+    (25, 0): [("tm_quant", 1, 3)],
 }
-EV = "sssssssv"
 
-FLOPS = 2 * B * HI * W * C * NO + 2 * B * NP * ND * W + 2 * B * NP * W * NO
+FLOPS = 2 * B * HEIGHTS * W * C * NO + 2 * B * CELLS * ND * W + 2 * B * CELLS * W * NO
 
 
 def tile_matrixvtringraybev_kernel(tc, x_bytes, x_scale, wc, gw, dl, gd, ring, ray, out):
@@ -111,16 +127,16 @@ def tile_matrixvtringraybev_kernel(tc, x_bytes, x_scale, wc, gw, dl, gd, ring, r
         def bank(tag, bufs):
             return psum.tile([P, 512], F32, name=tag, tag=tag, bufs=bufs)
 
-        def tp_bank():
+        def turn_bank():
             return bank("tp", 3)
-
-        def o_bank():
-            return bank("o", 2)
 
         def y_bank():
             return bank("y", 2)
 
-        def r_bank():
+        def rd_bank():
+            return bank("o", 2)
+
+        def out_bank():
             return bank("r", 1)
 
         ident = sb("ident", [P, P], F32)
@@ -130,99 +146,107 @@ def tile_matrixvtringraybev_kernel(tc, x_bytes, x_scale, wc, gw, dl, gd, ring, r
         warm = sb("warm", [P, 1], F32)
         nc.vector.memset(warm[:], 0.0)
 
-        scol = sb("scol", [P, 2, 4], F32)
-        nc.sync.dma_start(out=scol[:], in_=x_scale.rearrange("a b c (h p t) -> p (a b c h) t", h=2, t=4))
-        gd_b = sb("gd_b", [P, 4], BF16)
-        nc.scalar.dma_start(out=gd_b[:], in_=gd.rearrange("(p t) -> p t", t=4))
-        gw_b = sb("gw_b", [P, 4], BF16)
-        nc.scalar.dma_start(out=gw_b[:], in_=gw.rearrange("(p t) -> p t", t=4))
+        x_cols = sb("scol", [P, 2, PACK], F32)
+        nc.sync.dma_start(out=x_cols[:], in_=x_scale.rearrange("a b c (g p t) -> p (a b c g) t", g=2, t=PACK))
+        gd_b = sb("gd_b", [P, PACK], BF16)
+        nc.scalar.dma_start(out=gd_b[:], in_=gd.rearrange("(p t) -> p t", t=PACK))
+        gw_b = sb("gw_b", [P, PACK], BF16)
+        nc.scalar.dma_start(out=gw_b[:], in_=gw.rearrange("(p t) -> p t", t=PACK))
         nc.scalar.activation(out=warm[:], in_=warm[:], func=ACT.Exp)
 
-        wc_raw = [sb("wr", [P, 4, NO], BF16, bufs=2) for g in range(2)]
-        wc_v = wc.rearrange("(g p t) o -> g p t o", p=P, t=4)
-        xb = [[sb("xb%d%d" % (b, t), [P, HI, C], U8) for t in range(4)] for b in range(B)]
-        x_v = [x_bytes[b].rearrange("h (p t) k -> p t h k", t=4) for b in range(B)]
-        dl_raw = sb("dl_raw", [P, B * 4, ND], BF16)
-        dl_v = [dl[b].rearrange("(p t) n -> p t n", t=4) for b in range(B)]
-        ring_raw = sb("ring_raw", [P, 8, ND], BF16)
+        wc_raw = [sb("wr", [P, PACK, NO], BF16, bufs=2) for g in range(2)]
+        x_raw = [[sb("xb%d%d" % (b, t), [P, HEIGHTS, C], U8) for t in range(PACK)] for b in range(B)]
+        dl_raw = sb("dl_raw", [P, B * PACK, ND], BF16)
+        ring_raw = sb("ring_raw", [P, CHUNKS, ND], BF16)
         ray_raw = []
 
+        def load_wc(g):
+            nc.sync.dma_start(out=wc_raw[g][:], in_=wc.rearrange("(g p t) o -> g p t o", p=P, t=PACK)[g])
+
         def load_x(b, t, h0, h1):
-            nc.sync.dma_start(out=xb[b][t][:, h0:h1, :], in_=x_v[b][:, t, h0:h1, :])
+            rows = x_bytes[b].rearrange("h (p t) k -> p t h k", t=PACK)
+            nc.sync.dma_start(out=x_raw[b][t][:, h0:h1, :], in_=rows[:, t, h0:h1, :])
 
         def load_dl(b):
-            nc.sync.dma_start(out=dl_raw[:, 4 * b : 4 * b + 4, :], in_=dl_v[b])
+            nc.sync.dma_start(out=dl_raw[:, PACK * b : PACK * b + PACK, :], in_=dl[b].rearrange("(p t) n -> p t n", t=PACK))
 
-        load_x(0, 0, 0, 2)
-        nc.sync.dma_start(out=wc_raw[0][:], in_=wc_v[0])
+        def load_ray():
+            for i in range(2):
+                ray_raw.append(sb("wr", [P, PACK, W], BF16, bufs=2))
+                nc.sync.dma_start(
+                    out=ray_raw[i][:], in_=ray.rearrange("(p c) w -> p c w", c=CHUNKS)[:, 4 * i : 4 * i + 4, :]
+                )
+
+        load_x(0, 0, 0, 1)
+        load_wc(0)
+        load_x(0, 0, 1, 2)
+        load_wc(1)
         load_x(0, 0, 2, 4)
-        nc.sync.dma_start(out=wc_raw[1][:], in_=wc_v[1])
         load_dl(0)
         load_dl(1)
         load_x(0, 1, 0, 4)
         load_x(0, 2, 0, 4)
-        nc.sync.dma_start(out=ring_raw[:], in_=ring.rearrange("(p c) n -> p c n", c=8))
+        nc.sync.dma_start(out=ring_raw[:], in_=ring.rearrange("(p c) n -> p c n", c=CHUNKS))
         load_x(0, 3, 0, 4)
-        for t in range(4):
+        for t in range(PACK):
             load_x(1, t, 0, 4)
 
+        def spread(bank_ap, cols):
+            for t in range(PACK):
+                nc.tensor.transpose(bank_ap[:, t * P : (t + 1) * P], cols[:, t : t + 1].to_broadcast([P, P]), ident[:])
+
         scale = sb("scale", [P, C], F32)
-        for h in range(2):
-            sp = tp_bank()
-            for t in range(4):
-                nc.tensor.transpose(sp[:, t * P : (t + 1) * P], scol[:, h, t : t + 1].to_broadcast([P, P]), ident[:])
-            dst = scale[:, h * 512 : (h + 1) * 512].rearrange("q (p t) -> q p t", t=4)
-            src = sp[:].rearrange("q (t p) -> q p t", t=4)
-            if h == 0:
+        for g in range(2):
+            bk = turn_bank()
+            spread(bk, x_cols[:, g, :])
+            dst = scale[:, g * PASS : (g + 1) * PASS].rearrange("q (p t) -> q p t", t=PACK)
+            src = bk[:].rearrange("q (t p) -> q p t", t=PACK)
+            if g == 0:
                 nc.vector.tensor_copy(out=dst, in_=src)
             else:
                 nc.scalar.copy(out=dst, in_=src)
 
-        gd_f = sb("gd_f", [P, 4], F32)
-        nc.vector.tensor_copy(out=gd_f[:], in_=gd_b[:])
-        gw_f = sb("gw_f", [P, 4], F32)
-        nc.vector.tensor_copy(out=gw_f[:], in_=gw_b[:])
+        gd_f = sb("gd_f", [P, PACK], F32)
+        nc.gpsimd.tensor_copy(out=gd_f[:], in_=gd_b[:])
+        gw_f = sb("gw_f", [P, PACK], F32)
+        nc.gpsimd.tensor_copy(out=gw_f[:], in_=gw_b[:])
         gd_row = sb("gd_row", [P, ND], F32)
-        gp = tp_bank()
-        for t in range(4):
-            nc.tensor.transpose(gp[:, t * P : (t + 1) * P], gd_f[:, t : t + 1].to_broadcast([P, P]), ident[:])
-        nc.scalar.activation(
-            out=gd_row[:].rearrange("q (p t) -> q p t", t=4),
-            in_=gp[:].rearrange("q (t p) -> q p t", t=4),
-            func=ACT.Copy,
-            scale=float(ND),
-        )
+
+        def gd_spread():
+            bk = turn_bank()
+            spread(bk, gd_f)
+            nc.scalar.activation(
+                out=gd_row[:].rearrange("q (p t) -> q p t", t=PACK),
+                in_=bk[:].rearrange("q (t p) -> q p t", t=PACK),
+                func=ACT.Copy,
+                scale=float(ND),
+            )
 
         wq = sb("wq", [P, 2 * NO], U32)
         wq_s = sb("wq_s", [P, 2 * NO], U8)
-        wg = {}
-        nmax = sb("nmax", [P, B * 4], F32)
-        esum = [sb("esum%d" % b, [P, 4], F32) for b in range(B)]
-        rsum = [sb("rsum%d" % b, [P, 4], F32) for b in range(B)]
-        dg = {}
+        wc_mixed = {}
+        neg_max = sb("nmax", [P, B * PACK], F32)
+        exp_sum = [sb("esum%d" % b, [P, PACK], F32) for b in range(B)]
+        inv_sum = [sb("rsum%d" % b, [P, PACK], F32) for b in range(B)]
+        d_mixed = {}
         dq = [sb("dq%d" % b, [P, W], U32) for b in range(B)]
         dq_s = [sb("dq_s%d" % b, [P, W], U8) for b in range(B)]
-        rg = sb("rg", [P, NP * 4], BF16)
-        rq = sb("rq", [P, NP], U32)
-        rq_s = sb("rq_s", [P, NP], U8)
-        rayg = sb("rayg", [P, NP * 4], BF16)
-        tmg = {}
+        ring_mixed = sb("rg", [P, CELLS * PACK], BF16)
+        rq = sb("rq", [P, CELLS], U32)
+        rq_s = sb("rq_s", [P, CELLS], U8)
+        ray_mixed = sb("rayg", [P, CELLS * PACK], BF16)
+        tm_mixed = {}
         tq = [[sb("tq%d%d" % (b, i), [P, 512], U32) for i in range(2)] for b in range(B)]
         tq_s = [[sb("tq_s%d%d" % (b, i), [P, 512], U8) for i in range(2)] for b in range(B)]
-        msum = [[sb("msum%d%d" % (b, t), [P, 1], F32) for t in range(4)] for b in range(B)]
-        nbias = [[sb("nbias%d%d" % (b, t), [P, 1], F32) for t in range(4)] for b in range(B)]
-        cx = [sb("cx%d" % b, [P, 4, NO], BF16) for b in range(B)]
-        cg = [[sb("cg%d%d" % (b, i), [P, 1024], BF16) for i in range(2)] for b in range(B)]
+        m_sum = [[sb("msum%d%d" % (b, t), [P, 1], F32) for t in range(PACK)] for b in range(B)]
+        m_shift = [[sb("nbias%d%d" % (b, t), [P, 1], F32) for t in range(PACK)] for b in range(B)]
+        ctx_rows = [sb("cx%d" % b, [P, PACK, NO], BF16) for b in range(B)]
+        ctx_mixed = [[sb("cg%d%d" % (b, i), [P, 1024], BF16) for i in range(2)] for b in range(B)]
         cq = [[sb("cq%d%d" % (b, i), [P, 256], U32) for i in range(2)] for b in range(B)]
         cq_s = [[sb("cq_s%d%d" % (b, i), [P, 256], U8) for i in range(2)] for b in range(B)]
-        e_t = {}
-        d_t = {}
-        m_t = {}
-        o_t = {}
-        xs_t = {}
-        xg_t = {}
-        xq_t = {}
-        y_t = {}
+        exp_rows, d_rows, m_rows, rd_banks = {}, {}, {}, {}
+        x_rows, x_mixed, xq, y_banks = {}, {}, {}, {}
+        f_rows, f_banks, f_planes, f_mixed, fq = {}, {}, {}, {}, {}
 
         def quantize(codes, scales, src):
             nc.vector.quantize_mx(out=codes.bitcast(FP8X4), scales=scales, in_=src)
@@ -232,52 +256,54 @@ def tile_matrixvtringraybev_kernel(tc, x_bytes, x_scale, wc, gw, dl, gd, ring, r
                 out=dst, lhsT=lhs.bitcast(FP8X4), lhsT_scale=lhs_s, rhs=rhs.bitcast(FP8X4), rhs_scale=rhs_s, start=start, stop=stop
             )
 
-        def wc_interleave(g):
-            wg[g] = sb("fg", [P, NO * 4], BF16, bufs=2, pool=work)
-            nc.scalar.copy(out=wg[g][:].rearrange("p (o t) -> p o t", t=4), in_=wc_raw[g][:].rearrange("p t o -> p o t"))
+        def wc_mix(g):
+            wc_mixed[g] = sb("fg", [P, NO * PACK], BF16, bufs=2, pool=work)
+            nc.scalar.copy(out=wc_mixed[g][:].rearrange("p (o t) -> p o t", t=PACK), in_=wc_raw[g][:].rearrange("p t o -> p o t"))
 
         def wc_quant(g):
-            quantize(wq[:, g * NO : (g + 1) * NO], wq_s[:, g * NO : (g + 1) * NO], wg[g][:])
+            cols = slice(g * NO, (g + 1) * NO)
+            quantize(wq[:, cols], wq_s[:, cols], wc_mixed[g][:])
 
-        lev = [dl_raw]
+        halves = [dl_raw]
 
-        def dmax(i):
+        def dl_max(i):
             if i < 4:
                 n = ND >> (i + 1)
-                nxt = sb("lev%d" % i, [P, B * 4, n], BF16)
-                nc.vector.tensor_tensor(out=nxt[:], in0=lev[i][:, :, 0:n], in1=lev[i][:, :, n : 2 * n], op=ALU.max)
-                lev.append(nxt)
+                nxt = sb("lev%d" % i, [P, B * PACK, n], BF16)
+                nc.vector.tensor_tensor(out=nxt[:], in0=halves[i][:, :, 0:n], in1=halves[i][:, :, n : 2 * n], op=ALU.max)
+                halves.append(nxt)
             elif i == 4:
-                top = sb("dtop", [P, B * 4], F32)
-                nc.vector.tensor_reduce(out=top[:], in_=lev[4][:], axis=AXIS.X, op=ALU.max)
-                lev.append(top)
+                top = sb("dtop", [P, B * PACK], F32)
+                nc.vector.tensor_reduce(out=top[:], in_=halves[4][:], axis=AXIS.X, op=ALU.max)
+                halves.append(top)
             else:
-                nc.vector.tensor_scalar(out=nmax[:], in0=lev[5][:], scalar1=-1.0, scalar2=None, op0=ALU.mult)
+                nc.vector.tensor_scalar(out=neg_max[:], in0=halves[5][:], scalar1=-1.0, scalar2=None, op0=ALU.mult)
 
-        def dexp(b, t):
+        def dl_exp(b, t):
             e = sb("e", [P, ND], F32, bufs=4, pool=work)
-            r = 4 * b + t
+            r = PACK * b + t
             nc.scalar.activation(
-                out=e[:], in_=dl_raw[:, r, :], func=ACT.Exp, bias=nmax[:, r : r + 1], accum_out=esum[b][:, t : t + 1]
+                out=e[:], in_=dl_raw[:, r, :], func=ACT.Exp, bias=neg_max[:, r : r + 1], accum_out=exp_sum[b][:, t : t + 1]
             )
-            e_t[b, t] = e
+            exp_rows[b, t] = e
 
-        def drecip(b):
-            nc.vector.reciprocal(out=rsum[b][:], in_=esum[b][:])
+        def d_inv(b):
+            nc.vector.reciprocal(out=inv_sum[b][:], in_=exp_sum[b][:])
 
-        def dprod(b, t):
+        def d_prod(b, t):
             d = sb("d", [P, ND], BF16, bufs=4, pool=work)
             nc.vector.scalar_tensor_tensor(
-                out=d[:], in0=e_t[b, t][:], scalar=rsum[b][:, t : t + 1], in1=gd_row[:], op0=ALU.mult, op1=ALU.mult
+                out=d[:], in0=exp_rows[b, t][:], scalar=inv_sum[b][:, t : t + 1], in1=gd_row[:], op0=ALU.mult, op1=ALU.mult
             )
-            d_t[b, t] = d
+            d_rows[b, t] = d
 
-        def turn_pair(rows, dst):
-            bk = tp_bank()
+        def turn_two(rows, dst):
+            bk = turn_bank()
             for i in range(2):
                 words = rows[i].bitcast(F32)
                 for u in range(2):
-                    nc.tensor.transpose(bk[:, (2 * i + u) * P : (2 * i + u + 1) * P], words[:, u : 256 : 2], ident[:])
+                    at = (2 * i + u) * P
+                    nc.tensor.transpose(bk[:, at : at + P], words[:, u : ND // 2 : 2], ident[:])
             nc.scalar.copy(
                 out=dst.bitcast(F32).rearrange("p (i r u) -> p i r u", i=2, u=2),
                 in_=bk[:].rearrange("p (i u r) -> p i r u", i=2, u=2),
@@ -285,290 +311,283 @@ def tile_matrixvtringraybev_kernel(tc, x_bytes, x_scale, wc, gw, dl, gd, ring, r
 
         def d_turn(b, i):
             if i == 0:
-                dg[b] = sb("dg", [P, 4 * P * 4], BF16)
-            turn_pair([d_t[b, 2 * i][:], d_t[b, 2 * i + 1][:]], dg[b][:, i * 1024 : (i + 1) * 1024])
+                d_mixed[b] = sb("dg", [P, W * PACK], BF16)
+            turn_two([d_rows[b, 2 * i][:], d_rows[b, 2 * i + 1][:]], d_mixed[b][:, i * 1024 : (i + 1) * 1024])
 
         def d_quant(b):
-            quantize(dq[b][:], dq_s[b][:], dg[b][:])
+            quantize(dq[b][:], dq_s[b][:], d_mixed[b][:])
 
         def ring_turn(i):
-            turn_pair([ring_raw[:, 2 * i, :], ring_raw[:, 2 * i + 1, :]], rg[:, i * 1024 : (i + 1) * 1024])
+            turn_two([ring_raw[:, 2 * i, :], ring_raw[:, 2 * i + 1, :]], ring_mixed[:, i * 1024 : (i + 1) * 1024])
 
         def ring_quant(i):
-            quantize(rq[:, i * 512 : (i + 1) * 512], rq_s[:, i * 512 : (i + 1) * 512], rg[:, i * 2048 : (i + 1) * 2048])
-
-        def load_ray():
-            for i in range(2):
-                ray_raw.append(sb("wr", [P, 4, W], BF16, bufs=2))
-                nc.sync.dma_start(out=ray_raw[i][:], in_=ray.rearrange("(p c) w -> p c w", c=8)[:, 4 * i : 4 * i + 4, :])
+            cols = slice(i * 512, (i + 1) * 512)
+            quantize(rq[:, cols], rq_s[:, cols], ring_mixed[:, i * 2048 : (i + 1) * 2048])
 
         def ray_turn(i):
             half = ray_raw[i // 2]
             c = 2 * (i % 2)
-            turn_pair([half[:, c, :], half[:, c + 1, :]], rayg[:, i * 1024 : (i + 1) * 1024])
+            turn_two([half[:, c, :], half[:, c + 1, :]], ray_mixed[:, i * 1024 : (i + 1) * 1024])
 
-        def mm2(b, c):
-            o = y_bank() if (b, c) in ((1, 4), (1, 5)) else o_bank()
-            for t in range(4):
+        def rd_mm(b, c):
+            bk = y_bank() if (b, c) in ((1, 4), (1, 5)) else rd_bank()
+            for t in range(PACK):
                 sl = slice(t * P, (t + 1) * P)
                 cs = slice(c * P, (c + 1) * P)
-                mx(o[:, sl], dq[b][:, sl], dq_s[b][:, sl], rq[:, cs], rq_s[:, cs])
-            o_t[b, c] = o
+                mx(bk[:, sl], dq[b][:, sl], dq_s[b][:, sl], rq[:, cs], rq_s[:, cs])
+            rd_banks[b, c] = bk
 
-        def tm(b, c):
+        def tm_prod(b, c):
             i, r = divmod(c, 4)
             if r == 0:
-                tmg[b, i] = sb("tmg", [P, 2048], BF16, bufs=2)
+                tm_mixed[b, i] = sb("tmg", [P, 4 * P * PACK], BF16, bufs=2)
             nc.vector.tensor_tensor(
-                out=tmg[b, i][:, r * 512 : (r + 1) * 512].rearrange("p (n t) -> p n t", t=4),
-                in0=o_t[b, c][:].rearrange("p (t n) -> p n t", t=4),
-                in1=rayg[:, c * 512 : (c + 1) * 512].rearrange("p (n t) -> p n t", t=4),
+                out=tm_mixed[b, i][:, r * 512 : (r + 1) * 512].rearrange("p (n t) -> p n t", t=PACK),
+                in0=rd_banks[b, c][:].rearrange("p (t n) -> p n t", t=PACK),
+                in1=ray_mixed[:, c * 512 : (c + 1) * 512].rearrange("p (n t) -> p n t", t=PACK),
                 op=ALU.mult,
             )
 
         def tm_quant(b, q):
             i, h = divmod(q, 2)
             sl = slice(h * 256, (h + 1) * 256)
-            quantize(tq[b][i][:, sl], tq_s[b][i][:, sl], tmg[b, i][:, h * 1024 : (h + 1) * 1024])
+            quantize(tq[b][i][:, sl], tq_s[b][i][:, sl], tm_mixed[b, i][:, h * 1024 : (h + 1) * 1024])
 
-        def negmean(b, t):
-            (nc.vector if (b, t) == (1, 3) else nc.gpsimd).tensor_scalar(
-                out=nbias[b][t][:], in0=msum[b][t][:], scalar1=-1.0 / NO, scalar2=gw_f[:, t : t + 1], op0=ALU.mult, op1=ALU.mult
+        def ctx_shift(b, t, engine):
+            engine.tensor_scalar(
+                out=m_shift[b][t][:], in0=m_sum[b][t][:], scalar1=-1.0 / NO, scalar2=gw_f[:, t : t + 1], op0=ALU.mult, op1=ALU.mult
             )
 
-        def centre(b, t, eng):
-            if eng == "s":
-                nc.scalar.activation(out=cx[b][:, t, :], in_=m_t[b, t][:], func=ACT.Identity, bias=nbias[b][t][:], scale=gw_f[:, t : t + 1])
-            else:
-                nc.vector.tensor_scalar(
-                    out=cx[b][:, t, :], in0=m_t[b, t][:], scalar1=gw_f[:, t : t + 1], scalar2=nbias[b][t][:], op0=ALU.mult, op1=ALU.add
-                )
+        def ctx_centre(b, t):
+            nc.scalar.activation(
+                out=ctx_rows[b][:, t, :], in_=m_rows[b, t][:], func=ACT.Identity, bias=m_shift[b][t][:], scale=gw_f[:, t : t + 1]
+            )
 
-        def ctx_interleave(b, i, eng):
-            dst = cg[b][i][:].rearrange("p (o t) -> p o t", t=4)
-            src = cx[b][:, :, i * 256 : (i + 1) * 256].rearrange("p t o -> p o t")
-            if eng == "s":
-                nc.scalar.copy(out=dst, in_=src)
-            else:
-                nc.vector.tensor_copy(out=dst, in_=src)
+        def ctx_centre_last(b, t):
+            nc.vector.tensor_scalar(
+                out=ctx_rows[b][:, t, :],
+                in0=m_rows[b, t][:],
+                scalar1=gw_f[:, t : t + 1],
+                scalar2=m_shift[b][t][:],
+                op0=ALU.mult,
+                op1=ALU.add,
+            )
+
+        def ctx_mix(b, i, copy):
+            copy(
+                out=ctx_mixed[b][i][:].rearrange("p (o t) -> p o t", t=PACK),
+                in_=ctx_rows[b][:, :, i * 256 : (i + 1) * 256].rearrange("p t o -> p o t"),
+            )
 
         def ctx_quant(b, i):
-            quantize(cq[b][i][:], cq_s[b][i][:], cg[b][i][:])
+            quantize(cq[b][i][:], cq_s[b][i][:], ctx_mixed[b][i][:])
 
-        out_v = [out[b].rearrange("(p c) o -> p c o", c=8) for b in range(B)]
-
-        def mm3(b, c, eng, bk):
+        def out_mm(b, c, parts):
             i, r = divmod(c, 4)
             sl = slice(r * P, (r + 1) * P)
-            for n in range(2):
-                mx(bk[:, n * 256 : (n + 1) * 256], tq[b][i][:, sl], tq_s[b][i][:, sl], cq[b][n][:], cq_s[b][n][:])
-            res = sb("res", [P, NO], F32, bufs=8, pool=work)
-            if eng == "s":
-                nc.scalar.copy(out=res[:], in_=bk[:])
-            else:
-                nc.vector.tensor_copy(out=res[:], in_=bk[:])
-            nc.sync.dma_start(out=out_v[b][:, c, :], in_=res[:])
+            n = NO // len(parts)
+            rows = out[b].rearrange("(p c) o -> p c o", c=CHUNKS)
+            for q, (bk, copy) in enumerate(parts):
+                for k in range(q * n // 256, (q + 1) * n // 256):
+                    at = k * 256 - q * n
+                    mx(bk[:, at : at + 256], tq[b][i][:, sl], tq_s[b][i][:, sl], cq[b][k][:], cq_s[b][k][:])
+                res = sb("res", [P, NO], F32, bufs=8, pool=work)
+                copy(out=res[:, 0:n], in_=bk[:, 0:n])
+                nc.sync.dma_start(out=rows[:, c, q * n : (q + 1) * n], in_=res[:, 0:n])
 
         def where(j):
             return j // 8, (j // 2) % 4, 2 * (j % 2)
 
-        def is_scalar(b, t, g):
-            return (b, t, g) in BY_SCALAR
+        def vector_passes(j):
+            b, t, h0 = where(j)
+            return [g for g in range(2) if (b, t, g) not in BY_SCALAR]
 
         def x_mult(j, i):
             b, t, h0 = where(j)
-            cols = [g for g in range(2) if not is_scalar(b, t, g)]
-            if not cols:
-                return
-            lo, hi = cols[0] * 512, cols[-1] * 512 + 512
-            xs = sb("xs", [P, C], BF16, bufs=5, pool=work)
-            for c0, c1 in [(lo, 512), (512, hi)] if (j, i) == (0, 0) else [(lo, hi)]:
-                nc.vector.tensor_tensor(out=xs[:, c0:c1], in0=xb[b][t][:, h0 + i, c0:c1].bitcast(FP8), in1=scale[:, c0:c1], op=ALU.mult)
-            xs_t[j, i] = xs
+            passes = vector_passes(j)
+            lo, hi = passes[0] * PASS, passes[-1] * PASS + PASS
+            cuts = [(lo, PASS), (PASS, hi)] if (j, i) == (0, 0) else [(lo, hi)]
+            rows = sb("xs", [P, C], BF16, bufs=5, pool=work)
+            for k0, k1 in cuts:
+                nc.vector.tensor_tensor(
+                    out=rows[:, k0:k1], in0=x_raw[b][t][:, h0 + i, k0:k1].bitcast(FP8), in1=scale[:, k0:k1], op=ALU.mult
+                )
+            x_rows[j, i] = rows
 
         def x_turn(j, i):
-            b, t, h0 = where(j)
-            cols = [g for g in range(2) if not is_scalar(b, t, g)]
-            if not cols:
-                return
-            n = len(cols)
+            passes = vector_passes(j)
+            n = len(passes)
             if i == 0:
-                xg_t[j] = sb("xg", [P, 2 * 2 * P * 4], BF16, bufs=3, pool=work)
-            bk = tp_bank()
-            words = xs_t[j, i][:].bitcast(F32)
-            for s, g in enumerate(cols):
+                x_mixed[j] = sb("xg", [P, 2 * 2 * P * PACK], BF16, bufs=3, pool=work)
+            bk = turn_bank()
+            words = x_rows[j, i][:].bitcast(F32)
+            for s, g in enumerate(passes):
                 for u in range(2):
                     at = (2 * s + u) * P
                     nc.tensor.transpose(bk[:, at : at + P], words[:, 256 * g + u : 256 * (g + 1) : 2], ident[:])
             nc.scalar.copy(
-                out=xg_t[j][:].bitcast(F32)[:, i * n * 256 : (i + 1) * n * 256].rearrange("p (g r u) -> p g r u", g=n, u=2),
+                out=x_mixed[j][:].bitcast(F32)[:, i * n * 256 : (i + 1) * n * 256].rearrange("p (g r u) -> p g r u", g=n, u=2),
                 in_=bk[:, 0 : n * 256].rearrange("p (g u r) -> p g r u", g=n, u=2),
             )
 
         def x_quant(j, i0=0, i1=2):
-            b, t, h0 = where(j)
-            n = len([g for g in range(2) if not is_scalar(b, t, g)]) * P
-            if n == 0:
-                return
+            n = len(vector_passes(j)) * P
             if i0 == 0:
-                xq_t[j] = (sb("xq", [P, 512], U32, bufs=3, pool=work), sb("xq_s", [P, 512], U8, bufs=3, pool=work))
-            codes, scales = xq_t[j]
-            quantize(codes[:, i0 * n : i1 * n], scales[:, i0 * n : i1 * n], xg_t[j][:, 4 * i0 * n : 4 * i1 * n])
-
-        fc_t = {}
-        fb_t = {}
-        fp_t = {}
-        fg_t = {}
-        fq_t = {}
+                xq[j] = (sb("xq", [P, 512], U32, bufs=3, pool=work), sb("xq_s", [P, 512], U8, bufs=3, pool=work))
+            codes, scales = xq[j]
+            quantize(codes[:, i0 * n : i1 * n], scales[:, i0 * n : i1 * n], x_mixed[j][:, PACK * i0 * n : PACK * i1 * n])
 
         def f_cast(b, t, g, h):
             if h == 0:
-                fc_t[b, t, g] = sb("fc", [P, HI, 512], BF16, bufs=1, pool=work)
-            nc.scalar.copy(out=fc_t[b, t, g][:, h, :], in_=xb[b][t][:, h, g * 512 : (g + 1) * 512].bitcast(FP8))
+                f_rows[b, t, g] = sb("fc", [P, HEIGHTS, PASS], BF16, bufs=1, pool=work)
+            nc.scalar.copy(out=f_rows[b, t, g][:, h, :], in_=x_raw[b][t][:, h, g * PASS : (g + 1) * PASS].bitcast(FP8))
 
         def f_turn(b, t, g, v):
             bk = psum.tile([P, 1024], BF16, name="tp", tag="tp", bufs=3)
             for s in range(2):
-                for h in range(HI):
+                for h in range(HEIGHTS):
                     at = s * 512 + h * P
-                    nc.tensor.transpose(bk[:, at : at + P], fc_t[b, t, g][:, h, 2 * v + s : 512 : 4], ident_b[:])
-            fb_t[b, t, g, v] = bk
+                    nc.tensor.transpose(bk[:, at : at + P], f_rows[b, t, g][:, h, 2 * v + s : PASS : PACK], ident_b[:])
+            f_banks[b, t, g, v] = bk
 
         def f_scale(b, t, g, k):
             if k == 0:
-                fp_t[b, t, g] = sb("fp", [P, 4, 512], BF16, bufs=1, pool=work)
+                f_planes[b, t, g] = sb("fp", [P, PACK, 512], BF16, bufs=1, pool=work)
             nc.scalar.activation(
-                out=fp_t[b, t, g][:, k, :],
-                in_=fb_t[b, t, g, k // 2][:, (k % 2) * 512 : (k % 2 + 1) * 512],
+                out=f_planes[b, t, g][:, k, :],
+                in_=f_banks[b, t, g, k // 2][:, (k % 2) * 512 : (k % 2 + 1) * 512],
                 func=ACT.Copy,
-                scale=scol[:, g, k : k + 1],
+                scale=x_cols[:, g, k : k + 1],
             )
 
         def f_mix(b, t, g, n):
             if n == 0:
-                fg_t[b, t, g] = sb("fg", [P, 2048], BF16, bufs=2, pool=work)
-            rows = slice(n * 256, (n + 1) * 256)
+                f_mixed[b, t, g] = sb("fg", [P, 2048], BF16, bufs=2, pool=work)
             nc.scalar.copy(
-                out=fg_t[b, t, g][:, n * 1024 : (n + 1) * 1024].rearrange("p (r k) -> p r k", k=4),
-                in_=fp_t[b, t, g][:, :, rows].rearrange("p k r -> p r k"),
+                out=f_mixed[b, t, g][:, n * 1024 : (n + 1) * 1024].rearrange("p (r k) -> p r k", k=PACK),
+                in_=f_planes[b, t, g][:, :, n * 256 : (n + 1) * 256].rearrange("p k r -> p r k"),
             )
 
         def f_quant(b, t, g):
             codes, scales = sb("fq", [P, 512], U32, bufs=2, pool=work), sb("fq_s", [P, 512], U8, bufs=2, pool=work)
-            quantize(codes[:], scales[:], fg_t[b, t, g][:])
-            fq_t[b, t, g] = (codes, scales)
+            quantize(codes[:], scales[:], f_mixed[b, t, g][:])
+            fq[b, t, g] = (codes, scales)
 
-        def mm1(j, i0=0, i1=2):
+        def y_mm(j, i0=0, i1=2):
             b, t, h0 = where(j)
-            cols = [g for g in range(2) if not is_scalar(b, t, g)]
-            ys = y_t.setdefault(j, [])
+            passes = vector_passes(j)
+            ys = y_banks.setdefault(j, [])
             for i in range(i0, i1):
-                y = bank("y", 2)
+                y = y_bank()
                 for g in range(2):
-                    if g in cols:
-                        codes, scales = xq_t[j]
-                        at = (len(cols) * i + cols.index(g)) * P
+                    if g in passes:
+                        codes, scales = xq[j]
+                        at = (len(passes) * i + passes.index(g)) * P
                     else:
-                        codes, scales = fq_t[b, t, g]
+                        codes, scales = fq[b, t, g]
                         at = (h0 + i) * P
                     sl = slice(at, at + P)
-                    ocols = slice(g * NO, (g + 1) * NO)
-                    mx(y[:], codes[:, sl], scales[:, sl], wq[:, ocols], wq_s[:, ocols], start=g == 0, stop=g == 1)
+                    oc = slice(g * NO, (g + 1) * NO)
+                    mx(y[:], codes[:, sl], scales[:, sl], wq[:, oc], wq_s[:, oc], start=g == 0, stop=g == 1)
                 ys.append(y)
             if h0 == 0 and i0 == 0:
                 m = sb("m", [P, NO], F32, bufs=4, pool=work)
                 nc.scalar.copy(out=m[:], in_=ys[0][:])
-                m_t[b, t] = m
+                m_rows[b, t] = m
 
-        def max_a(j):
+        def max_first(j):
             b, t, h0 = where(j)
             if h0 == 2:
-                nc.vector.tensor_tensor(out=m_t[b, t][:], in0=y_t[j][0][:], in1=m_t[b, t][:], op=ALU.max)
+                nc.vector.tensor_tensor(out=m_rows[b, t][:], in0=y_banks[j][0][:], in1=m_rows[b, t][:], op=ALU.max)
 
-        def max_b(j):
+        def max_second(j):
             b, t, h0 = where(j)
-            m = m_t[b, t]
-            y = y_t[j][1]
+            m = m_rows[b, t]
+            y = y_banks[j][1]
             if h0 == 0:
                 nc.vector.tensor_tensor(out=m[:], in0=y[:], in1=m[:], op=ALU.max)
             else:
                 nc.vector.scalar_tensor_tensor(
-                    out=m[:], in0=y[:], scalar=1.0, in1=m[:], op0=ALU.mult, op1=ALU.max, accum_out=msum[b][t][:]
+                    out=m[:], in0=y[:], scalar=1.0, in1=m[:], op0=ALU.mult, op1=ALU.max, accum_out=m_sum[b][t][:]
                 )
 
-        def mean_b(j, eng="s"):
-            b, t, h0 = where(j)
-            if h0 == 2:
-                negmean(b, t)
-                centre(b, t, eng)
-
-        def run(items):
-            for item in items:
-                item[0](*item[1:])
-
-        def ctx_il_s(b, i):
-            ctx_interleave(b, i, "s")
-
-        def mm3_s(b, c):
-            mm3(b, c, "s", r_bank())
-
-        def mean_item(b, t):
-            negmean(b, t)
-
-        def centre_item(b, t):
-            centre(b, t, "s")
-
-        FN = {
-            "dmax": dmax, "ringq": ring_quant, "recip": drecip, "dprod": dprod, "dq": d_quant, "tm": tm, "tmq": tm_quant,
-            "fq": f_quant, "cq": ctx_quant, "wq": wc_quant, "mm2": mm2, "ring": ring_turn, "ray": ray_turn, "exp": dexp,
-            "dt": d_turn, "fc": f_cast, "ft": f_turn, "fs": f_scale, "fm": f_mix, "ci": ctx_il_s, "mm3": mm3_s, "wi": wc_interleave,
-            "mean": mean_item, "centre": centre_item,
+        STEPS = {
+            "wc_mix": wc_mix,
+            "wc_quant": wc_quant,
+            "gd_spread": gd_spread,
+            "dl_max": dl_max,
+            "dl_exp": dl_exp,
+            "d_inv": d_inv,
+            "d_prod": d_prod,
+            "d_turn": d_turn,
+            "d_quant": d_quant,
+            "ring_turn": ring_turn,
+            "ring_quant": ring_quant,
+            "ray_turn": ray_turn,
+            "rd_mm": rd_mm,
+            "tm_prod": tm_prod,
+            "tm_quant": tm_quant,
+            "ctx_shift": lambda b, t: ctx_shift(b, t, nc.gpsimd),
+            "ctx_centre": ctx_centre,
+            "ctx_mix": lambda b, i: ctx_mix(b, i, nc.scalar.copy),
+            "ctx_quant": ctx_quant,
+            "out_mm": lambda b, c: out_mm(b, c, [(out_bank(), nc.scalar.copy)]),
+            "f_cast": f_cast,
+            "f_turn": f_turn,
+            "f_scale": f_scale,
+            "f_mix": f_mix,
+            "f_quant": f_quant,
         }
 
-        def at(j, p):
-            for item in PLAN.get((j, p), []):
-                FN[item[0]](*item[1:])
+        def other(step, place):
+            for entry in OTHER_WORK.get((step, place), []):
+                STEPS[entry[0]](*entry[1:])
 
-        n_pairs = 16
-        for j in range(18):
-            x = j < n_pairs
+        for j in range(PAIRS + 2):
+            streaming = j < PAIRS
             if j == 2:
                 load_ray()
-            at(j, 0)
-            if x:
+            other(j, 0)
+            if streaming:
                 x_mult(j, 0)
-            at(j, 1)
+            other(j, 1)
             if j >= 2:
-                max_a(j - 2)
-            if x:
+                max_first(j - 2)
+            if streaming:
                 x_mult(j, 1)
-            if 1 <= j < 16:
+            if 1 <= j < PAIRS:
                 x_quant(j - 1)
-            elif j == 16:
-                x_quant(15, 0, 1)
-            if x:
+            elif j == PAIRS:
+                x_quant(j - 1, 0, 1)
+            if streaming:
                 x_turn(j, 0)
-            at(j, 2)
-            if x:
+            other(j, 2)
+            if streaming:
                 x_turn(j, 1)
-            at(j, 3)
+            other(j, 3)
             if j >= 2:
-                max_b(j - 2)
-            if 1 <= j < 16:
-                mm1(j - 1)
-            elif j == 16:
-                mm1(15, 0, 1)
-                x_quant(15, 1, 2)
-                mm1(15, 1, 2)
-            at(j, 4)
-        mean_b(n_pairs - 1, "v")
-        at(18, 0)
-        ctx_interleave(1, 0, "v")
-        ctx_interleave(1, 1, "s")
-        at(18, 1)
-        ctx_quant(1, 0)
-        ctx_quant(1, 1)
-        at(18, 2)
-        for c in range(8):
-            at(19 + c, 0)
-            mm3(1, c, EV[c], (tp_bank, tp_bank, r_bank)[c % 3]())
+                max_second(j - 2)
+            if 1 <= j < PAIRS:
+                y_mm(j - 1)
+            elif j == PAIRS:
+                y_mm(j - 1, 0, 1)
+                x_quant(j - 1, 1, 2)
+                y_mm(j - 1, 1, 2)
+            other(j, 4)
+
+        step = PAIRS + 2
+        ctx_shift(B - 1, PACK - 1, nc.vector)
+        ctx_centre_last(B - 1, PACK - 1)
+        other(step, 0)
+        ctx_mix(B - 1, 0, nc.vector.tensor_copy)
+        ctx_mix(B - 1, 1, nc.scalar.copy)
+        other(step, 1)
+        ctx_quant(B - 1, 0)
+        ctx_quant(B - 1, 1)
+        other(step, 2)
+        for c in range(CHUNKS):
+            other(step + 1 + c, 0)
+            if c < CHUNKS - 1:
+                out_mm(B - 1, c, [((turn_bank, turn_bank, out_bank)[c % 3](), nc.scalar.copy)])
+            else:
+                out_mm(B - 1, c, [(turn_bank(), nc.scalar.copy), (out_bank(), nc.vector.tensor_copy)])

from contextlib import ExitStack

import concourse.mybir as mybir
from concourse.masks import make_identity

F32 = mybir.dt.float32
BF16 = mybir.dt.bfloat16
U32 = mybir.dt.uint32
U8 = mybir.dt.uint8
FP8 = mybir.dt.float8_e4m3fn
FP8X4 = mybir.dt.float8_e4m3fn_x4
ACT = mybir.ActivationFunctionType
ALU = mybir.AluOpType
AXIS = mybir.AxisListType

P = 128
PACK = 4
PASS = P * PACK
B = 2
HEIGHTS = 4
W = 512
C = 1024
ND = 512
CELLS = 1024
CHUNKS = CELLS // P
NO = 512
PAIRS = B * PACK * HEIGHTS // 2

BY_SCALAR = ((1, 1, 0), (1, 3, 0),)

OTHER_WORK = {
    (0, 0): [("wc_mix", 0)],
    (0, 4): [("gd_spread",)],
    (1, 1): [("wc_mix", 1)],
    (1, 2): [("dl_max", 0), ("dl_max", 1), ("wc_quant", 0), ("dl_max", 2), ("wc_quant", 1)],
    (1, 3): [("dl_max", 3)],
    (1, 4): [("ring_turn", 2)],
    (2, 1): [("dl_max", 4)],
    (2, 2): [("dl_max", 5)],
    (2, 3): [("dl_exp", 0, 3)],
    (2, 4): [("dl_exp", 0, 1)],
    (3, 0): [("dl_exp", 0, 2), ("dl_exp", 0, 0)],
    (3, 1): [("ring_turn", 3)],
    (3, 2): [("d_inv", 0), ("ring_turn", 0)],
    (3, 3): [("f_cast", 1, 1, 0, 0), ("f_cast", 1, 1, 0, 2)],
    (3, 4): [("ray_turn", 2), ("d_prod", 0, 0)],
    (4, 2): [("f_cast", 1, 1, 0, 3)],
    (4, 3): [("d_prod", 0, 3), ("dl_exp", 1, 1), ("d_prod", 0, 1)],
    (5, 0): [("ring_turn", 1), ("f_cast", 1, 1, 0, 1)],
    (5, 1): [("d_turn", 0, 0)],
    (5, 3): [("d_prod", 0, 2), ("dl_exp", 1, 3), ("ring_quant", 1)],
    (5, 4): [("ring_quant", 0), ("dl_exp", 1, 0), ("dl_exp", 1, 2)],
    (6, 0): [("f_turn", 1, 1, 0, 0), ("f_scale", 1, 1, 0, 0), ("f_scale", 1, 1, 0, 1)],
    (6, 1): [("ctx_shift", 0, 1)],
    (6, 2): [("d_turn", 0, 1)],
    (6, 3): [("ctx_centre", 0, 1), ("d_inv", 1)],
    (6, 4): [("d_prod", 1, 3), ("f_turn", 1, 1, 0, 1)],
    (7, 0): [("f_scale", 1, 1, 0, 2)],
    (7, 1): [("d_prod", 1, 0), ("d_prod", 1, 1), ("f_cast", 1, 3, 0, 0), ("f_scale", 1, 1, 0, 3)],
    (7, 2): [("ray_turn", 0), ("ctx_shift", 0, 0)],
    (7, 3): [("d_prod", 1, 2)],
    (7, 4): [("d_quant", 0), ("rd_mm", 0, 0)],
    (8, 0): [("f_mix", 1, 1, 0, 0), ("f_cast", 1, 3, 0, 3)],
    (8, 2): [("ray_turn", 1)],
    (8, 3): [("tm_prod", 0, 0)],
    (8, 4): [("f_mix", 1, 1, 0, 1), ("ctx_centre", 0, 0), ("d_turn", 1, 0), ("rd_mm", 0, 2)],
    (9, 1): [("rd_mm", 0, 1), ("ctx_shift", 0, 2), ("d_turn", 1, 1)],
    (9, 2): [("f_quant", 1, 1, 0)],
    (9, 4): [("tm_prod", 0, 2), ("ctx_shift", 0, 3)],
    (10, 0): [("ctx_centre", 0, 3), ("ray_turn", 3), ("tm_prod", 0, 1)],
    (10, 2): [("ctx_centre", 0, 2), ("f_cast", 1, 3, 0, 1), ("rd_mm", 0, 3)],
    (10, 3): [("d_quant", 1)],
    (10, 4): [("f_cast", 1, 3, 0, 2), ("rd_mm", 0, 4)],
    (11, 0): [("ctx_mix", 0, 0)],
    (11, 1): [("tm_prod", 0, 3)],
    (11, 2): [
        ("tm_quant", 0, 1), ("tm_prod", 0, 4), ("ctx_mix", 0, 1), ("f_turn", 1, 3, 0, 1), ("f_turn", 1, 3, 0, 0),
        ("f_scale", 1, 3, 0, 0), ("f_scale", 1, 3, 0, 2),
    ],
    (11, 3): [("f_scale", 1, 3, 0, 3)],
    (12, 0): [("ctx_quant", 0, 0), ("f_scale", 1, 3, 0, 1), ("tm_quant", 0, 0)],
    (12, 1): [("ctx_shift", 1, 0), ("rd_mm", 0, 7), ("ctx_quant", 0, 1)],
    (12, 2): [("f_mix", 1, 3, 0, 0)],
    (13, 0): [("f_mix", 1, 3, 0, 1)],
    (13, 1): [("out_mm", 0, 0)],
    (13, 2): [("tm_prod", 0, 7)],
    (13, 4): [("rd_mm", 0, 5)],
    (14, 0): [("rd_mm", 0, 6)],
    (14, 1): [("out_mm", 0, 1)],
    (14, 3): [("ctx_centre", 1, 0)],
    (14, 4): [("f_quant", 1, 3, 0)],
    (15, 0): [("tm_prod", 0, 5), ("rd_mm", 1, 0)],
    (15, 1): [("out_mm", 0, 3)],
    (15, 3): [("out_mm", 0, 2)],
    (15, 4): [("tm_prod", 0, 6), ("rd_mm", 1, 1)],
    (16, 0): [("tm_quant", 0, 2), ("tm_quant", 0, 3)],
    (16, 1): [("ctx_shift", 1, 2)],
    (16, 2): [("ctx_centre", 1, 2), ("tm_prod", 1, 0), ("out_mm", 0, 7)],
    (16, 4): [("ctx_shift", 1, 1), ("ctx_centre", 1, 1), ("out_mm", 0, 5)],
    (17, 0): [("rd_mm", 1, 2)],
    (17, 2): [("tm_prod", 1, 1), ("out_mm", 0, 4)],
    (17, 3): [("rd_mm", 1, 3)],
    (17, 4): [("rd_mm", 1, 5), ("tm_prod", 1, 2), ("rd_mm", 1, 4)],
    (18, 0): [("tm_prod", 1, 3)],
    (18, 1): [("tm_quant", 1, 0)],
    (18, 2): [("out_mm", 0, 6), ("tm_quant", 1, 1), ("tm_prod", 1, 4)],
    (19, 0): [("tm_prod", 1, 5), ("rd_mm", 1, 7)],
    (20, 0): [("tm_prod", 1, 7)],
    (21, 0): [("rd_mm", 1, 6), ("tm_quant", 1, 2), ("tm_prod", 1, 6)],
    (25, 0): [("tm_quant", 1, 3)],
}

FLOPS = 2 * B * HEIGHTS * W * C * NO + 2 * B * CELLS * ND * W + 2 * B * CELLS * W * NO


def tile_matrixvtringraybev_kernel(tc, x_bytes, x_scale, wc, gw, dl, gd, ring, ray, out):
    nc = tc.nc
    with ExitStack() as ctx:
        keep = ctx.enter_context(tc.tile_pool(name="keep", bufs=1))
        work = ctx.enter_context(tc.tile_pool(name="work", bufs=1))
        psum = ctx.enter_context(tc.psum_pool(name="psum", bufs=1))
        ctx.enter_context(tc.manual_schedule())

        def sb(name, shape, dtype, bufs=1, pool=keep):
            return pool.tile(shape, dtype, name=name, tag=name, bufs=bufs, align_bytes=64)

        def bank(tag, bufs):
            return psum.tile([P, 512], F32, name=tag, tag=tag, bufs=bufs)

        def turn_bank():
            return bank("tp", 3)

        def y_bank():
            return bank("y", 2)

        def rd_bank():
            return bank("o", 2)

        def out_bank():
            return bank("r", 1)

        ident = sb("ident", [P, P], F32)
        make_identity(nc, ident[:])
        ident_b = sb("ident_b", [P, P], BF16)
        nc.gpsimd.tensor_copy(out=ident_b[:], in_=ident[:])
        warm = sb("warm", [P, 1], F32)
        nc.vector.memset(warm[:], 0.0)

        x_cols = sb("scol", [P, 2, PACK], F32)
        nc.sync.dma_start(out=x_cols[:], in_=x_scale.rearrange("a b c (g p t) -> p (a b c g) t", g=2, t=PACK))
        gd_b = sb("gd_b", [P, PACK], BF16)
        nc.scalar.dma_start(out=gd_b[:], in_=gd.rearrange("(p t) -> p t", t=PACK))
        gw_b = sb("gw_b", [P, PACK], BF16)
        nc.scalar.dma_start(out=gw_b[:], in_=gw.rearrange("(p t) -> p t", t=PACK))
        nc.scalar.activation(out=warm[:], in_=warm[:], func=ACT.Exp)

        wc_raw = [sb("wr", [P, PACK, NO], BF16, bufs=2) for g in range(2)]
        x_raw = [[sb("xb%d%d" % (b, t), [P, HEIGHTS, C], U8) for t in range(PACK)] for b in range(B)]
        dl_raw = sb("dl_raw", [P, B * PACK, ND], BF16)
        ring_raw = sb("ring_raw", [P, CHUNKS, ND], BF16)
        ray_raw = []

        def load_wc(g):
            nc.sync.dma_start(out=wc_raw[g][:], in_=wc.rearrange("(g p t) o -> g p t o", p=P, t=PACK)[g])

        def load_x(b, t, h0, h1):
            rows = x_bytes[b].rearrange("h (p t) k -> p t h k", t=PACK)
            nc.sync.dma_start(out=x_raw[b][t][:, h0:h1, :], in_=rows[:, t, h0:h1, :])

        def load_dl(b):
            nc.sync.dma_start(out=dl_raw[:, PACK * b : PACK * b + PACK, :], in_=dl[b].rearrange("(p t) n -> p t n", t=PACK))

        def load_ray():
            for i in range(2):
                ray_raw.append(sb("wr", [P, PACK, W], BF16, bufs=2))
                nc.sync.dma_start(
                    out=ray_raw[i][:], in_=ray.rearrange("(p c) w -> p c w", c=CHUNKS)[:, 4 * i : 4 * i + 4, :]
                )

        load_x(0, 0, 0, 1)
        load_wc(0)
        load_x(0, 0, 1, 2)
        load_wc(1)
        load_x(0, 0, 2, 4)
        load_dl(0)
        load_dl(1)
        load_x(0, 1, 0, 4)
        load_x(0, 2, 0, 4)
        nc.sync.dma_start(out=ring_raw[:], in_=ring.rearrange("(p c) n -> p c n", c=CHUNKS))
        load_x(0, 3, 0, 4)
        for t in range(PACK):
            load_x(1, t, 0, 4)

        def spread(bank_ap, cols):
            for t in range(PACK):
                nc.tensor.transpose(bank_ap[:, t * P : (t + 1) * P], cols[:, t : t + 1].to_broadcast([P, P]), ident[:])

        scale = sb("scale", [P, C], F32)
        for g in range(2):
            bk = turn_bank()
            spread(bk, x_cols[:, g, :])
            dst = scale[:, g * PASS : (g + 1) * PASS].rearrange("q (p t) -> q p t", t=PACK)
            src = bk[:].rearrange("q (t p) -> q p t", t=PACK)
            if g == 0:
                nc.vector.tensor_copy(out=dst, in_=src)
            else:
                nc.scalar.copy(out=dst, in_=src)

        gd_f = sb("gd_f", [P, PACK], F32)
        nc.gpsimd.tensor_copy(out=gd_f[:], in_=gd_b[:])
        gw_f = sb("gw_f", [P, PACK], F32)
        nc.gpsimd.tensor_copy(out=gw_f[:], in_=gw_b[:])
        gd_row = sb("gd_row", [P, ND], F32)

        def gd_spread():
            bk = turn_bank()
            spread(bk, gd_f)
            nc.scalar.activation(
                out=gd_row[:].rearrange("q (p t) -> q p t", t=PACK),
                in_=bk[:].rearrange("q (t p) -> q p t", t=PACK),
                func=ACT.Copy,
                scale=float(ND),
            )

        wq = sb("wq", [P, 2 * NO], U32)
        wq_s = sb("wq_s", [P, 2 * NO], U8)
        wc_mixed = {}
        neg_max = sb("nmax", [P, B * PACK], F32)
        exp_sum = [sb("esum%d" % b, [P, PACK], F32) for b in range(B)]
        inv_sum = [sb("rsum%d" % b, [P, PACK], F32) for b in range(B)]
        d_mixed = {}
        dq = [sb("dq%d" % b, [P, W], U32) for b in range(B)]
        dq_s = [sb("dq_s%d" % b, [P, W], U8) for b in range(B)]
        ring_mixed = sb("rg", [P, CELLS * PACK], BF16)
        rq = sb("rq", [P, CELLS], U32)
        rq_s = sb("rq_s", [P, CELLS], U8)
        ray_mixed = sb("rayg", [P, CELLS * PACK], BF16)
        tm_mixed = {}
        tq = [[sb("tq%d%d" % (b, i), [P, 512], U32) for i in range(2)] for b in range(B)]
        tq_s = [[sb("tq_s%d%d" % (b, i), [P, 512], U8) for i in range(2)] for b in range(B)]
        m_sum = [[sb("msum%d%d" % (b, t), [P, 1], F32) for t in range(PACK)] for b in range(B)]
        m_shift = [[sb("nbias%d%d" % (b, t), [P, 1], F32) for t in range(PACK)] for b in range(B)]
        ctx_rows = [sb("cx%d" % b, [P, PACK, NO], BF16) for b in range(B)]
        ctx_mixed = [[sb("cg%d%d" % (b, i), [P, 1024], BF16) for i in range(2)] for b in range(B)]
        cq = [[sb("cq%d%d" % (b, i), [P, 256], U32) for i in range(2)] for b in range(B)]
        cq_s = [[sb("cq_s%d%d" % (b, i), [P, 256], U8) for i in range(2)] for b in range(B)]
        exp_rows, d_rows, m_rows, rd_banks = {}, {}, {}, {}
        x_rows, x_mixed, xq, y_banks = {}, {}, {}, {}
        f_rows, f_banks, f_planes, f_mixed, fq = {}, {}, {}, {}, {}

        def quantize(codes, scales, src):
            nc.vector.quantize_mx(out=codes.bitcast(FP8X4), scales=scales, in_=src)

        def mx(dst, lhs, lhs_s, rhs, rhs_s, start=True, stop=True):
            nc.tensor.matmul_mx(
                out=dst, lhsT=lhs.bitcast(FP8X4), lhsT_scale=lhs_s, rhs=rhs.bitcast(FP8X4), rhs_scale=rhs_s, start=start, stop=stop
            )

        def wc_mix(g):
            wc_mixed[g] = sb("fg", [P, NO * PACK], BF16, bufs=2, pool=work)
            nc.scalar.copy(out=wc_mixed[g][:].rearrange("p (o t) -> p o t", t=PACK), in_=wc_raw[g][:].rearrange("p t o -> p o t"))

        def wc_quant(g):
            cols = slice(g * NO, (g + 1) * NO)
            quantize(wq[:, cols], wq_s[:, cols], wc_mixed[g][:])

        halves = [dl_raw]

        def dl_max(i):
            if i < 4:
                n = ND >> (i + 1)
                nxt = sb("lev%d" % i, [P, B * PACK, n], BF16)
                nc.vector.tensor_tensor(out=nxt[:], in0=halves[i][:, :, 0:n], in1=halves[i][:, :, n : 2 * n], op=ALU.max)
                halves.append(nxt)
            elif i == 4:
                top = sb("dtop", [P, B * PACK], F32)
                nc.vector.tensor_reduce(out=top[:], in_=halves[4][:], axis=AXIS.X, op=ALU.max)
                halves.append(top)
            else:
                nc.vector.tensor_scalar(out=neg_max[:], in0=halves[5][:], scalar1=-1.0, scalar2=None, op0=ALU.mult)

        def dl_exp(b, t):
            e = sb("e", [P, ND], F32, bufs=4, pool=work)
            r = PACK * b + t
            nc.scalar.activation(
                out=e[:], in_=dl_raw[:, r, :], func=ACT.Exp, bias=neg_max[:, r : r + 1], accum_out=exp_sum[b][:, t : t + 1]
            )
            exp_rows[b, t] = e

        def d_inv(b):
            nc.vector.reciprocal(out=inv_sum[b][:], in_=exp_sum[b][:])

        def d_prod(b, t):
            d = sb("d", [P, ND], BF16, bufs=4, pool=work)
            nc.vector.scalar_tensor_tensor(
                out=d[:], in0=exp_rows[b, t][:], scalar=inv_sum[b][:, t : t + 1], in1=gd_row[:], op0=ALU.mult, op1=ALU.mult
            )
            d_rows[b, t] = d

        def turn_two(rows, dst):
            bk = turn_bank()
            for i in range(2):
                words = rows[i].bitcast(F32)
                for u in range(2):
                    at = (2 * i + u) * P
                    nc.tensor.transpose(bk[:, at : at + P], words[:, u : ND // 2 : 2], ident[:])
            nc.scalar.copy(
                out=dst.bitcast(F32).rearrange("p (i r u) -> p i r u", i=2, u=2),
                in_=bk[:].rearrange("p (i u r) -> p i r u", i=2, u=2),
            )

        def d_turn(b, i):
            if i == 0:
                d_mixed[b] = sb("dg", [P, W * PACK], BF16)
            turn_two([d_rows[b, 2 * i][:], d_rows[b, 2 * i + 1][:]], d_mixed[b][:, i * 1024 : (i + 1) * 1024])

        def d_quant(b):
            quantize(dq[b][:], dq_s[b][:], d_mixed[b][:])

        def ring_turn(i):
            turn_two([ring_raw[:, 2 * i, :], ring_raw[:, 2 * i + 1, :]], ring_mixed[:, i * 1024 : (i + 1) * 1024])

        def ring_quant(i):
            cols = slice(i * 512, (i + 1) * 512)
            quantize(rq[:, cols], rq_s[:, cols], ring_mixed[:, i * 2048 : (i + 1) * 2048])

        def ray_turn(i):
            half = ray_raw[i // 2]
            c = 2 * (i % 2)
            turn_two([half[:, c, :], half[:, c + 1, :]], ray_mixed[:, i * 1024 : (i + 1) * 1024])

        def rd_mm(b, c):
            bk = y_bank() if (b, c) in ((1, 4), (1, 5)) else rd_bank()
            for t in range(PACK):
                sl = slice(t * P, (t + 1) * P)
                cs = slice(c * P, (c + 1) * P)
                mx(bk[:, sl], dq[b][:, sl], dq_s[b][:, sl], rq[:, cs], rq_s[:, cs])
            rd_banks[b, c] = bk

        def tm_prod(b, c):
            i, r = divmod(c, 4)
            if r == 0:
                tm_mixed[b, i] = sb("tmg", [P, 4 * P * PACK], BF16, bufs=2)
            nc.vector.tensor_tensor(
                out=tm_mixed[b, i][:, r * 512 : (r + 1) * 512].rearrange("p (n t) -> p n t", t=PACK),
                in0=rd_banks[b, c][:].rearrange("p (t n) -> p n t", t=PACK),
                in1=ray_mixed[:, c * 512 : (c + 1) * 512].rearrange("p (n t) -> p n t", t=PACK),
                op=ALU.mult,
            )

        def tm_quant(b, q):
            i, h = divmod(q, 2)
            sl = slice(h * 256, (h + 1) * 256)
            quantize(tq[b][i][:, sl], tq_s[b][i][:, sl], tm_mixed[b, i][:, h * 1024 : (h + 1) * 1024])

        def ctx_shift(b, t, engine):
            engine.tensor_scalar(
                out=m_shift[b][t][:], in0=m_sum[b][t][:], scalar1=-1.0 / NO, scalar2=gw_f[:, t : t + 1], op0=ALU.mult, op1=ALU.mult
            )

        def ctx_centre(b, t):
            nc.scalar.activation(
                out=ctx_rows[b][:, t, :], in_=m_rows[b, t][:], func=ACT.Identity, bias=m_shift[b][t][:], scale=gw_f[:, t : t + 1]
            )

        def ctx_centre_last(b, t):
            nc.vector.tensor_scalar(
                out=ctx_rows[b][:, t, :],
                in0=m_rows[b, t][:],
                scalar1=gw_f[:, t : t + 1],
                scalar2=m_shift[b][t][:],
                op0=ALU.mult,
                op1=ALU.add,
            )

        def ctx_mix(b, i, copy):
            copy(
                out=ctx_mixed[b][i][:].rearrange("p (o t) -> p o t", t=PACK),
                in_=ctx_rows[b][:, :, i * 256 : (i + 1) * 256].rearrange("p t o -> p o t"),
            )

        def ctx_quant(b, i):
            quantize(cq[b][i][:], cq_s[b][i][:], ctx_mixed[b][i][:])

        def out_mm(b, c, parts):
            i, r = divmod(c, 4)
            sl = slice(r * P, (r + 1) * P)
            n = NO // len(parts)
            rows = out[b].rearrange("(p c) o -> p c o", c=CHUNKS)
            for q, (bk, copy) in enumerate(parts):
                for k in range(q * n // 256, (q + 1) * n // 256):
                    at = k * 256 - q * n
                    mx(bk[:, at : at + 256], tq[b][i][:, sl], tq_s[b][i][:, sl], cq[b][k][:], cq_s[b][k][:])
                res = sb("res", [P, NO], F32, bufs=8, pool=work)
                copy(out=res[:, 0:n], in_=bk[:, 0:n])
                nc.sync.dma_start(out=rows[:, c, q * n : (q + 1) * n], in_=res[:, 0:n])

        def where(j):
            return j // 8, (j // 2) % 4, 2 * (j % 2)

        def vector_passes(j):
            b, t, h0 = where(j)
            return [g for g in range(2) if (b, t, g) not in BY_SCALAR]

        def x_mult(j, i):
            b, t, h0 = where(j)
            passes = vector_passes(j)
            lo, hi = passes[0] * PASS, passes[-1] * PASS + PASS
            cuts = [(lo, PASS), (PASS, hi)] if (j, i) == (0, 0) else [(lo, hi)]
            rows = sb("xs", [P, C], BF16, bufs=5, pool=work)
            for k0, k1 in cuts:
                nc.vector.tensor_tensor(
                    out=rows[:, k0:k1], in0=x_raw[b][t][:, h0 + i, k0:k1].bitcast(FP8), in1=scale[:, k0:k1], op=ALU.mult
                )
            x_rows[j, i] = rows

        def x_turn(j, i):
            passes = vector_passes(j)
            n = len(passes)
            if i == 0:
                x_mixed[j] = sb("xg", [P, 2 * 2 * P * PACK], BF16, bufs=3, pool=work)
            bk = turn_bank()
            words = x_rows[j, i][:].bitcast(F32)
            for s, g in enumerate(passes):
                for u in range(2):
                    at = (2 * s + u) * P
                    nc.tensor.transpose(bk[:, at : at + P], words[:, 256 * g + u : 256 * (g + 1) : 2], ident[:])
            nc.scalar.copy(
                out=x_mixed[j][:].bitcast(F32)[:, i * n * 256 : (i + 1) * n * 256].rearrange("p (g r u) -> p g r u", g=n, u=2),
                in_=bk[:, 0 : n * 256].rearrange("p (g u r) -> p g r u", g=n, u=2),
            )

        def x_quant(j, i0=0, i1=2):
            n = len(vector_passes(j)) * P
            if i0 == 0:
                xq[j] = (sb("xq", [P, 512], U32, bufs=3, pool=work), sb("xq_s", [P, 512], U8, bufs=3, pool=work))
            codes, scales = xq[j]
            quantize(codes[:, i0 * n : i1 * n], scales[:, i0 * n : i1 * n], x_mixed[j][:, PACK * i0 * n : PACK * i1 * n])

        def f_cast(b, t, g, h):
            if h == 0:
                f_rows[b, t, g] = sb("fc", [P, HEIGHTS, PASS], BF16, bufs=1, pool=work)
            nc.scalar.copy(out=f_rows[b, t, g][:, h, :], in_=x_raw[b][t][:, h, g * PASS : (g + 1) * PASS].bitcast(FP8))

        def f_turn(b, t, g, v):
            bk = psum.tile([P, 1024], BF16, name="tp", tag="tp", bufs=3)
            for s in range(2):
                for h in range(HEIGHTS):
                    at = s * 512 + h * P
                    nc.tensor.transpose(bk[:, at : at + P], f_rows[b, t, g][:, h, 2 * v + s : PASS : PACK], ident_b[:])
            f_banks[b, t, g, v] = bk

        def f_scale(b, t, g, k):
            if k == 0:
                f_planes[b, t, g] = sb("fp", [P, PACK, 512], BF16, bufs=1, pool=work)
            nc.scalar.activation(
                out=f_planes[b, t, g][:, k, :],
                in_=f_banks[b, t, g, k // 2][:, (k % 2) * 512 : (k % 2 + 1) * 512],
                func=ACT.Copy,
                scale=x_cols[:, g, k : k + 1],
            )

        def f_mix(b, t, g, n):
            if n == 0:
                f_mixed[b, t, g] = sb("fg", [P, 2048], BF16, bufs=2, pool=work)
            nc.scalar.copy(
                out=f_mixed[b, t, g][:, n * 1024 : (n + 1) * 1024].rearrange("p (r k) -> p r k", k=PACK),
                in_=f_planes[b, t, g][:, :, n * 256 : (n + 1) * 256].rearrange("p k r -> p r k"),
            )

        def f_quant(b, t, g):
            codes, scales = sb("fq", [P, 512], U32, bufs=2, pool=work), sb("fq_s", [P, 512], U8, bufs=2, pool=work)
            quantize(codes[:], scales[:], f_mixed[b, t, g][:])
            fq[b, t, g] = (codes, scales)

        def y_mm(j, i0=0, i1=2):
            b, t, h0 = where(j)
            passes = vector_passes(j)
            ys = y_banks.setdefault(j, [])
            for i in range(i0, i1):
                y = y_bank()
                for g in range(2):
                    if g in passes:
                        codes, scales = xq[j]
                        at = (len(passes) * i + passes.index(g)) * P
                    else:
                        codes, scales = fq[b, t, g]
                        at = (h0 + i) * P
                    sl = slice(at, at + P)
                    oc = slice(g * NO, (g + 1) * NO)
                    mx(y[:], codes[:, sl], scales[:, sl], wq[:, oc], wq_s[:, oc], start=g == 0, stop=g == 1)
                ys.append(y)
            if h0 == 0 and i0 == 0:
                m = sb("m", [P, NO], F32, bufs=4, pool=work)
                nc.scalar.copy(out=m[:], in_=ys[0][:])
                m_rows[b, t] = m

        def max_first(j):
            b, t, h0 = where(j)
            if h0 == 2:
                nc.vector.tensor_tensor(out=m_rows[b, t][:], in0=y_banks[j][0][:], in1=m_rows[b, t][:], op=ALU.max)

        def max_second(j):
            b, t, h0 = where(j)
            m = m_rows[b, t]
            y = y_banks[j][1]
            if h0 == 0:
                nc.vector.tensor_tensor(out=m[:], in0=y[:], in1=m[:], op=ALU.max)
            else:
                nc.vector.scalar_tensor_tensor(
                    out=m[:], in0=y[:], scalar=1.0, in1=m[:], op0=ALU.mult, op1=ALU.max, accum_out=m_sum[b][t][:]
                )

        STEPS = {
            "wc_mix": wc_mix,
            "wc_quant": wc_quant,
            "gd_spread": gd_spread,
            "dl_max": dl_max,
            "dl_exp": dl_exp,
            "d_inv": d_inv,
            "d_prod": d_prod,
            "d_turn": d_turn,
            "d_quant": d_quant,
            "ring_turn": ring_turn,
            "ring_quant": ring_quant,
            "ray_turn": ray_turn,
            "rd_mm": rd_mm,
            "tm_prod": tm_prod,
            "tm_quant": tm_quant,
            "ctx_shift": lambda b, t: ctx_shift(b, t, nc.gpsimd),
            "ctx_centre": ctx_centre,
            "ctx_mix": lambda b, i: ctx_mix(b, i, nc.scalar.copy),
            "ctx_quant": ctx_quant,
            "out_mm": lambda b, c: out_mm(b, c, [(out_bank(), nc.scalar.copy)]),
            "f_cast": f_cast,
            "f_turn": f_turn,
            "f_scale": f_scale,
            "f_mix": f_mix,
            "f_quant": f_quant,
        }

        def other(step, place):
            for entry in OTHER_WORK.get((step, place), []):
                STEPS[entry[0]](*entry[1:])

        for j in range(PAIRS + 2):
            streaming = j < PAIRS
            if j == 2:
                load_ray()
            other(j, 0)
            if streaming:
                x_mult(j, 0)
            other(j, 1)
            if j >= 2:
                max_first(j - 2)
            if streaming:
                x_mult(j, 1)
            if 1 <= j < PAIRS:
                x_quant(j - 1)
            elif j == PAIRS:
                x_quant(j - 1, 0, 1)
            if streaming:
                x_turn(j, 0)
            other(j, 2)
            if streaming:
                x_turn(j, 1)
            other(j, 3)
            if j >= 2:
                max_second(j - 2)
            if 1 <= j < PAIRS:
                y_mm(j - 1)
            elif j == PAIRS:
                y_mm(j - 1, 0, 1)
                x_quant(j - 1, 1, 2)
                y_mm(j - 1, 1, 2)
            other(j, 4)

        step = PAIRS + 2
        ctx_shift(B - 1, PACK - 1, nc.vector)
        ctx_centre_last(B - 1, PACK - 1)
        other(step, 0)
        ctx_mix(B - 1, 0, nc.vector.tensor_copy)
        ctx_mix(B - 1, 1, nc.scalar.copy)
        other(step, 1)
        ctx_quant(B - 1, 0)
        ctx_quant(B - 1, 1)
        other(step, 2)
        for c in range(CHUNKS):
            other(step + 1 + c, 0)
            if c < CHUNKS - 1:
                out_mm(B - 1, c, [((turn_bank, turn_bank, out_bank)[c % 3](), nc.scalar.copy)])
            else:
                out_mm(B - 1, c, [(turn_bank(), nc.scalar.copy), (out_bank(), nc.vector.tensor_copy)])
